import numpy as np
import ml_dtypes


def mxq(x, axis, fmt="e4m3"):
    dtype, down = {"e4m3": (ml_dtypes.float8_e4m3fn, 7), "e5m2": (ml_dtypes.float8_e5m2, 14)}[fmt]
    v = np.moveaxis(np.asarray(x, np.float32).astype(ml_dtypes.bfloat16).astype(np.float64), axis, -1)
    blocks = v.reshape(v.shape[:-1] + (-1, 32))
    amax = np.abs(blocks).max(-1, keepdims=True)
    byte = np.maximum(np.where(amax > 0, np.frexp(amax)[1] - 1 + 127, 0) - down, 1)
    scale = np.exp2(byte - 127.0)
    codes = (blocks / scale).astype(np.float32).astype(dtype).astype(np.float64)
    return np.moveaxis((codes * scale).reshape(v.shape), -1, axis)


WIDE = False


def mx_kscale(k):
    if not WIDE:
        return np.ones(k)
    levels = np.array([10, -10, 5, -5, 0])
    if k % 512:
        return np.exp2(np.random.permutation(np.resize(levels, k // 32))).repeat(32)
    a = np.empty((k // 512, 16))
    for p in range(k // 512):
        a[p, :8] = np.random.permutation(np.resize(levels, 8))
        for g in range(8):
            far = levels[np.abs(levels - a[p, g]) >= 10]
            a[p, g + 8] = far[np.random.randint(len(far))]
    return np.exp2(a.ravel()).repeat(32)


def f64(x):
    return np.asarray(x).astype(np.float64)


def striped(idx):
    return np.tile(idx.reshape(-1, 16).T, (8, 1)).astype(np.uint16)


def unstriped(offs):
    return offs[:16].T.reshape(-1).astype(np.int64)


E2M1 = np.array([0.0, 0.5, 1.0, 1.5, 2.0, 3.0, 4.0, 6.0, -0.0, -0.5, -1.0, -1.5, -2.0, -3.0, -4.0, -6.0])


def pack_weight(w, fmt):
    k, n = w.shape
    w = f64(np.asarray(w, np.float32).astype(ml_dtypes.bfloat16)).reshape(k // 32, 32, n)
    amax = np.abs(w).max(1)
    if fmt == "e4m3":
        byte = np.frexp(amax)[1] - 1 + 127 - 7
    else:
        mant, ex = np.frexp(amax / 6.0)
        byte = np.where(mant > 0.5, ex, ex - 1) + 127
    byte = np.clip(np.where(amax > 0, byte, 1), 1, 254)
    scaled = (w * np.exp2(127.0 - byte)[:, None, :]).reshape(k, n).astype(np.float32)
    by_word = np.ascontiguousarray(scaled.reshape(k // 512, 128, 4, n).transpose(0, 1, 3, 2))
    if fmt == "e4m3":
        words = by_word.astype(ml_dtypes.float8_e4m3fn).view(np.uint8)
    else:
        c = by_word.astype(ml_dtypes.float4_e2m1fn).view(np.uint8) & 0xF
        words = (c[..., 0::2] | (c[..., 1::2] << 4)).reshape(k // 512, 128, 2 * n)
    return np.ascontiguousarray(words), np.ascontiguousarray(byte.astype(np.uint8).reshape(k // 512, 16, n))


def unpack_weight(words, scales, fmt):
    g, _, n = scales.shape
    words = np.ascontiguousarray(words).reshape(g, 128, n, -1)
    if fmt == "e4m3":
        vals = words.view(ml_dtypes.float8_e4m3fn).astype(np.float64)
    else:
        nib = np.empty((g, 128, n, 4), np.uint8)
        nib[..., 0::2] = words & 0xF
        nib[..., 1::2] = words >> 4
        vals = E2M1[nib]
    vals = vals * np.repeat(np.exp2(scales.astype(np.float64) - 127.0), 8, axis=1)[..., None]
    return vals.transpose(0, 1, 3, 2).reshape(g * 512, n)


def relu(v):
    return np.maximum(v, 0.0)


K, T, E1, C1, E2, C2, H = 512, 512, 2, 256, 2, 256, 512
N = 128


def by_expert(wq, xq, E, C):
    return np.concatenate([wq[e].T @ xq[:, e * C:(e + 1) * C] for e in range(E)], axis=1)


def setup_inputs():
    n = np.random.standard_normal
    s = mx_kscale(K)
    u = mx_kscale(H)
    slots1, slots2 = np.random.permutation(T), np.random.permutation(T)
    x = pack_weight(n((K, T)) * s[:, None], "e4m3")
    wa = [pack_weight(m, "e4m3") for m in n((E1, K, H)) / np.sqrt(K) / s[None, :, None]]
    wb = [pack_weight(m, "e4m3") for m in n((E2, K, H)) / np.sqrt(K) / s[None, :, None] * u]
    w2 = pack_weight(n((H, N)) / np.sqrt(H) / u[:, None], "e4m3")
    return {
        "x_words": x[0],
        "x_scales": x[1],
        "wa_words": np.stack([m[0] for m in wa]),
        "wa_scales": np.stack([m[1] for m in wa]),
        "wb_words": np.stack([m[0] for m in wb]),
        "wb_scales": np.stack([m[1] for m in wb]),
        "w2_words": w2[0],
        "w2_scales": w2[1],
        "offs": striped(slots1),
        "offs2": striped(slots2),
    }


def reference(x_words, x_scales, wa_words, wa_scales, wb_words, wb_scales, w2_words, w2_scales, offs, offs2):
    wa = np.stack([unpack_weight(wa_words[e], wa_scales[e], "e4m3") for e in range(E1)])
    wb = np.stack([unpack_weight(wb_words[e], wb_scales[e], "e4m3") for e in range(E2)])
    w2 = unpack_weight(w2_words, w2_scales, "e4m3")
    idx, idx2 = unstriped(offs), unstriped(offs2)
    x = unpack_weight(x_words, x_scales, "e4m3")
    a, c = np.zeros((H, T)), np.zeros((H, T))
    a[:, idx] = by_expert(wa, x[:, idx], E1, C1)
    c[:, idx2] = by_expert(wb, x[:, idx2], E2, C2)
    return w2.T @ mxq(relu(a) * c, 0, "e4m3")

@@ -1,0 +1,193 @@
+from contextlib import ExitStack
+
+import concourse.mybir as mybir
+from concourse.masks import make_identity
+
+K, T, H, N = 512, 512, 512, 128
+E, C = 2, 256
+FLOPS = 2 * (2 * K * H * T) + 2 * H * N * T
+
+F32 = mybir.dt.float32
+BF16 = mybir.dt.bfloat16
+I32 = mybir.dt.int32
+U32 = mybir.dt.uint32
+U16 = mybir.dt.uint16
+U8 = mybir.dt.uint8
+FP8X4 = mybir.dt.float8_e4m3fn_x4
+RELU = mybir.ActivationFunctionType.Relu
+MULT = mybir.AluOpType.mult
+
+P = 128
+PACK = 4
+HALF = T // 2
+
+
+def tile_moe_pool_relu_kernel(tc, x_words, x_scales, wa_words, wa_scales, wb_words, wb_scales, w2_words, w2_scales, offs, offs2, out):
+    nc = tc.nc
+    with ExitStack() as ctx:
+        held = ctx.enter_context(tc.tile_pool(name="held", bufs=1))
+        ps_mm = ctx.enter_context(tc.psum_pool(name="ps_mm", bufs=2))
+        ps_tr = ctx.enter_context(tc.psum_pool(name="ps_tr", bufs=4))
+        ps_out = ctx.enter_context(tc.psum_pool(name="ps_out", bufs=1))
+
+        def load_words(name, dram, width):
+            tile = held.tile([P, width], I32, name=name, align_bytes=64)
+            nc.sync.dma_start(tile[:], dram.rearrange("p c d -> p (c d)").bitcast(I32))
+            return tile
+
+        def load_scales_repeated(name, dram, width, queue):
+            tile = held.tile([P, width], U8, name=name, align_bytes=64)
+            for q in range(4):
+                rows = dram[4 * q : 4 * q + 4, :].bitcast(I32).unsqueeze(0)
+                queue.dma_start(tile[32 * q : 32 * q + 32, :].bitcast(I32), rows.to_broadcast([8, 4, width // 4]))
+            return tile
+
+        def zeroed_plane(name):
+            tile = held.tile([P, H // 4], I32, name=name, align_bytes=64)
+            nc.vector.memset(tile[:], 0)
+            return tile
+
+        def load_pool_scales(tile, dram):
+            for q in range(4):
+                nc.sync.dma_start(tile[32 * q : 32 * q + 4 * E, :], dram[:, 0, 4 * q : 4 * q + 4, :].bitcast(I32))
+
+        lists = [held.tile([P, T // 16], U16, name="list_a"), held.tile([P, T // 16], U16, name="list_c")]
+        ww, ws = {}, {}
+        pool_planes = [zeroed_plane("was"), zeroed_plane("wbs")]
+        for pool in range(2):
+            for e in range(E):
+                ws[pool, e] = pool_planes[pool][4 * e :, :].bitcast(U8)
+        nc.sync.dma_start(lists[0][:], offs)
+        xw = load_words("xw", x_words[0], T)
+        xs = load_scales_repeated("xs", x_scales[0], T, nc.scalar)
+        ww[0, 0] = load_words("wa0", wa_words[0, 0], H)
+        load_pool_scales(pool_planes[0], wa_scales)
+        nc.sync.dma_start(lists[1][:], offs2)
+        ww[0, 1] = load_words("wa1", wa_words[1, 0], H)
+        ww[1, 0] = load_words("wb0", wb_words[0, 0], H)
+        load_pool_scales(pool_planes[1], wb_scales)
+        ww[1, 1] = load_words("wb1", wb_words[1, 0], H)
+        w2w = load_words("w2w", w2_words[0], N)
+        w2s = load_scales_repeated("w2s", w2_scales[0], N, nc.sync)
+
+        identity = held.tile([P, P], F32, name="identity", align_bytes=64)
+        make_identity(nc, identity[:])
+
+        def slots(pool, e):
+            return lists[pool][:, e * (C // 16) : (e + 1) * (C // 16)]
+
+        gathered = {}
+
+        def gather(pool, e):
+            words = held.tile([P, C], U32, name=f"g_words{pool}{e}", align_bytes=64)
+            scales = held.tile([P, C], U8, name=f"g_scales{pool}{e}", align_bytes=64)
+            nc.vector.tensor_copy(words[:], xw[:].bitcast(U32).indirect(slots(pool, e)))
+            nc.vector.tensor_copy(scales[:], xs[:].indirect(slots(pool, e)))
+            gathered[pool, e] = (words, scales)
+
+        rows = {}
+
+        def expert(pool, e):
+            words, scales = gathered[pool, e]
+            for b in range(C // P):
+                cols = slice(b * P, (b + 1) * P)
+                acc = ps_mm.tile([P, H], F32, name="acc")
+                nc.tensor.matmul_mx(
+                    out=acc[:],
+                    lhsT=words[:, cols].bitcast(FP8X4),
+                    lhsT_scale=scales[:, cols],
+                    rhs=ww[pool, e][:].bitcast(FP8X4),
+                    rhs_scale=ws[pool, e],
+                    start=True,
+                    stop=True,
+                )
+                row = held.tile([P, PACK, P], F32, name=f"row{pool}{e}{b}", align_bytes=64)
+                by_plane = acc[:].rearrange("s (p t) -> s t p", t=PACK)
+                if pool == 0:
+                    nc.scalar.activation(row[:], by_plane, RELU)
+                else:
+                    nc.scalar.copy(row[:], by_plane)
+                rows[pool, e, b] = row
+
+        windows = {}
+        for pool in range(2):
+            for t in range(PACK):
+                windows[pool, t] = held.tile([P, T], F32, name=f"window{pool}{t}", align_bytes=64)
+        turned = {}
+
+        def turn(pool, e, t):
+            bank = ps_tr.tile([P, C], F32, name="bank")
+            for b in range(C // P):
+                nc.tensor.transpose(bank[:, b * P : (b + 1) * P], rows[pool, e, b][:, t, :], identity[:])
+            src = held.tile([P, C], F32, name=f"src{pool}{e}{t}", align_bytes=64)
+            nc.scalar.copy(src[:], bank[:])
+            turned[pool, e, t] = src
+
+        def scatter(pool, e, t):
+            nc.vector.tensor_copy(windows[pool, t][:].indirect(slots(pool, e)), turned[pool, e, t][:])
+
+        planes = held.tile([P, PACK, T], BF16, name="planes", align_bytes=64)
+
+        def product(engine, t, cols):
+            engine.tensor_tensor(planes[:, t, cols], windows[0, t][:, cols], windows[1, t][:, cols], MULT)
+
+        gather(0, 0)
+        expert(0, 0)
+        gather(0, 1)
+        gather(1, 0)
+        gather(1, 1)
+
+        order = [
+            (0, 0, 0), (0, 0, 1), (0, 0, 2),
+            (0, 1, 0), (1, 0, 0), (0, 1, 1), (1, 1, 0),
+            (1, 0, 1), (0, 1, 2), (1, 1, 1),
+            (1, 0, 2), (0, 0, 3), (1, 1, 2),
+            (1, 0, 3), (0, 1, 3), (1, 1, 3),
+        ]
+        product_after = {7: 0, 10: 1, 13: 2}
+        experts_before = {1: (0, 1), 2: (1, 0), 4: (1, 1)}
+        for step, (pool, e, t) in enumerate(order):
+            if step in experts_before:
+                expert(*experts_before[step])
+            turn(pool, e, t)
+            scatter(pool, e, t)
+            if step in product_after:
+                product(nc.vector, product_after[step], slice(0, T))
+
+        halves = [slice(0, HALF), slice(HALF, T)]
+        product(nc.vector, PACK - 1, halves[1])
+        product(nc.vector, PACK - 1, halves[0])
+        grouped = []
+        for u in range(2):
+            tile = held.tile([P, HALF, PACK], BF16, name=f"grouped{u}", align_bytes=64)
+            dst = tile[:].rearrange("p (c i) t -> p c t i", i=4)
+            src = planes[:, :, halves[u]].rearrange("p t (c i) -> p c t i", i=4)
+            if u == 0:
+                nc.vector.tensor_copy(dst, src)
+            else:
+                nc.scalar.copy(dst, src)
+            grouped.append(tile)
+        for u in range(2):
+            h_words = held.tile([P, HALF], U32, name=f"h_words{u}", align_bytes=64)
+            h_scales = held.tile([P, HALF], U8, name=f"h_scales{u}", align_bytes=64)
+            nc.vector.quantize_mx(
+                out=h_words[:].bitcast(FP8X4),
+                scales=h_scales[:],
+                in_=grouped[u][:].rearrange("p c t -> p (c t)"),
+            )
+            total = ps_out.tile([N, HALF], F32, name=f"total{u}")
+            nc.tensor.matmul_mx(
+                out=total[:],
+                lhsT=w2w[:].bitcast(FP8X4),
+                lhsT_scale=w2s[:],
+                rhs=h_words[:].bitcast(FP8X4),
+                rhs_scale=h_scales[:],
+                start=True,
+                stop=True,
+            )
+            result = held.tile([N, HALF], F32, name=f"result{u}")
+            if u == 0:
+                nc.scalar.copy(result[:], total[:])
+            else:
+                nc.vector.tensor_copy(result[:], total[:])
+            nc.sync.dma_start(out[:, halves[u]], result[:])

@@ -19,7 +19,8 @@ MULT = mybir.AluOpType.mult
 
 P = 128
 PACK = 4
-HALF = T // 2
+WIDE = 704
+PART = 128
 
 
 def tile_moe_pool_relu_kernel(tc, x_words, x_scales, wa_words, wa_scales, wb_words, wb_scales, w2_words, w2_scales, offs, offs2, out):
@@ -27,12 +28,12 @@ def tile_moe_pool_relu_kernel(tc, x_words, x_scales, wa_words, wa_scales, wb_wor
     with ExitStack() as ctx:
         held = ctx.enter_context(tc.tile_pool(name="held", bufs=1))
         ps_mm = ctx.enter_context(tc.psum_pool(name="ps_mm", bufs=2))
-        ps_tr = ctx.enter_context(tc.psum_pool(name="ps_tr", bufs=4))
+        ps_tr = ctx.enter_context(tc.psum_pool(name="ps_tr", bufs=2))
         ps_out = ctx.enter_context(tc.psum_pool(name="ps_out", bufs=1))
 
-        def load_words(name, dram, width):
+        def load_words(name, dram, width, queue):
             tile = held.tile([P, width], I32, name=name, align_bytes=64)
-            nc.sync.dma_start(tile[:], dram.rearrange("p c d -> p (c d)").bitcast(I32))
+            queue.dma_start(tile[:], dram.rearrange("p c d -> p (c d)").bitcast(I32))
             return tile
 
         def load_scales_repeated(name, dram, width, queue):
@@ -44,12 +45,12 @@ def tile_moe_pool_relu_kernel(tc, x_words, x_scales, wa_words, wa_scales, wb_wor
 
         def zeroed_plane(name):
             tile = held.tile([P, H // 4], I32, name=name, align_bytes=64)
-            nc.vector.memset(tile[:], 0)
+            nc.gpsimd.memset(tile[:], 0)
             return tile
 
-        def load_pool_scales(tile, dram):
-            for q in range(4):
-                nc.sync.dma_start(tile[32 * q : 32 * q + 4 * E, :], dram[:, 0, 4 * q : 4 * q + 4, :].bitcast(I32))
+        def load_pool_scales(tile, dram, queues):
+            for q, queue in enumerate(queues):
+                queue.dma_start(tile[32 * q : 32 * q + 4 * E, :], dram[:, 0, 4 * q : 4 * q + 4, :].bitcast(I32))
 
         lists = [held.tile([P, T // 16], U16, name="list_a"), held.tile([P, T // 16], U16, name="list_c")]
         ww, ws = {}, {}
@@ -58,31 +59,31 @@ def tile_moe_pool_relu_kernel(tc, x_words, x_scales, wa_words, wa_scales, wb_wor
             for e in range(E):
                 ws[pool, e] = pool_planes[pool][4 * e :, :].bitcast(U8)
         nc.sync.dma_start(lists[0][:], offs)
-        xw = load_words("xw", x_words[0], T)
-        xs = load_scales_repeated("xs", x_scales[0], T, nc.scalar)
-        ww[0, 0] = load_words("wa0", wa_words[0, 0], H)
-        load_pool_scales(pool_planes[0], wa_scales)
+        xw = load_words("xw", x_words[0], T, nc.scalar)
+        xs = load_scales_repeated("xs", x_scales[0], T, nc.sync)
+        ww[0, 0] = load_words("wa0", wa_words[0, 0], H, nc.scalar)
+        load_pool_scales(pool_planes[0], wa_scales, [nc.gpsimd, nc.gpsimd, nc.gpsimd, nc.sync])
         nc.sync.dma_start(lists[1][:], offs2)
-        ww[0, 1] = load_words("wa1", wa_words[1, 0], H)
-        ww[1, 0] = load_words("wb0", wb_words[0, 0], H)
-        load_pool_scales(pool_planes[1], wb_scales)
-        ww[1, 1] = load_words("wb1", wb_words[1, 0], H)
-        w2w = load_words("w2w", w2_words[0], N)
+        ww[0, 1] = load_words("wa1", wa_words[1, 0], H, nc.sync)
+        ww[1, 0] = load_words("wb0", wb_words[0, 0], H, nc.sync)
+        load_pool_scales(pool_planes[1], wb_scales, [nc.sync] * 4)
+        ww[1, 1] = load_words("wb1", wb_words[1, 0], H, nc.sync)
+        w2w = load_words("w2w", w2_words[0], N, nc.sync)
         w2s = load_scales_repeated("w2s", w2_scales[0], N, nc.sync)
 
         identity = held.tile([P, P], F32, name="identity", align_bytes=64)
         make_identity(nc, identity[:])
 
-        def slots(pool, e):
-            return lists[pool][:, e * (C // 16) : (e + 1) * (C // 16)]
+        def slots(pool, blocks):
+            return lists[pool][:, blocks[0] * (P // 16) : (blocks[-1] + 1) * (P // 16)]
 
         gathered = {}
 
         def gather(pool, e):
             words = held.tile([P, C], U32, name=f"g_words{pool}{e}", align_bytes=64)
             scales = held.tile([P, C], U8, name=f"g_scales{pool}{e}", align_bytes=64)
-            nc.vector.tensor_copy(words[:], xw[:].bitcast(U32).indirect(slots(pool, e)))
-            nc.vector.tensor_copy(scales[:], xs[:].indirect(slots(pool, e)))
+            nc.vector.tensor_copy(scales[:], xs[:].indirect(slots(pool, [2 * e, 2 * e + 1])))
+            nc.vector.tensor_copy(words[:], xw[:].bitcast(U32).indirect(slots(pool, [2 * e, 2 * e + 1])))
             gathered[pool, e] = (words, scales)
 
         rows = {}
@@ -107,75 +108,80 @@ def tile_moe_pool_relu_kernel(tc, x_words, x_scales, wa_words, wa_scales, wb_wor
                     nc.scalar.activation(row[:], by_plane, RELU)
                 else:
                     nc.scalar.copy(row[:], by_plane)
-                rows[pool, e, b] = row
+                rows[pool, 2 * e + b] = row
 
         windows = {}
         for pool in range(2):
             for t in range(PACK):
-                windows[pool, t] = held.tile([P, T], F32, name=f"window{pool}{t}", align_bytes=64)
-        turned = {}
+                width = T if pool == 0 and t < 2 else WIDE
+                windows[pool, t] = held.tile([P, width], F32, name=f"window{pool}{t}", align_bytes=64)
 
-        def turn(pool, e, t):
-            bank = ps_tr.tile([P, C], F32, name="bank")
-            for b in range(C // P):
-                nc.tensor.transpose(bank[:, b * P : (b + 1) * P], rows[pool, e, b][:, t, :], identity[:])
-            src = held.tile([P, C], F32, name=f"src{pool}{e}{t}", align_bytes=64)
+        def put_back(pool, blocks, t):
+            width = P * len(blocks)
+            bank = ps_tr.tile([P, width], F32, name="bank")
+            for j, block in enumerate(blocks):
+                nc.tensor.transpose(bank[:, j * P : (j + 1) * P], rows[pool, block][:, t, :], identity[:])
+            src = held.tile([P, width], F32, name=f"src{pool}{blocks[0]}{t}", align_bytes=64)
             nc.scalar.copy(src[:], bank[:])
-            turned[pool, e, t] = src
-
-        def scatter(pool, e, t):
-            nc.vector.tensor_copy(windows[pool, t][:].indirect(slots(pool, e)), turned[pool, e, t][:])
+            nc.vector.tensor_copy(windows[pool, t][:].indirect(slots(pool, blocks)), src[:])
 
         planes = held.tile([P, PACK, T], BF16, name="planes", align_bytes=64)
 
         def product(engine, t, cols):
             engine.tensor_tensor(planes[:, t, cols], windows[0, t][:, cols], windows[1, t][:, cols], MULT)
 
+        both = [0, 1, 2, 3]
+        everyone = slice(0, T)
         gather(0, 0)
         expert(0, 0)
         gather(0, 1)
         gather(1, 0)
         gather(1, 1)
+        put_back(0, [0], 0)
+        put_back(0, [0], 1)
+        put_back(0, [1], 0)
+        expert(0, 1)
+        put_back(0, [1], 1)
+        put_back(0, [2, 3], 0)
+        expert(1, 0)
+        put_back(0, [2, 3], 1)
+        expert(1, 1)
+        put_back(0, both, 2)
+        put_back(1, both, 0)
+        product(nc.gpsimd, 0, everyone)
+        put_back(1, both, 1)
+        product(nc.gpsimd, 1, everyone)
+        put_back(1, both, 2)
+        product(nc.gpsimd, 2, everyone)
+        put_back(0, both, 3)
 
-        order = [
-            (0, 0, 0), (0, 0, 1), (0, 0, 2),
-            (0, 1, 0), (1, 0, 0), (0, 1, 1), (1, 1, 0),
-            (1, 0, 1), (0, 1, 2), (1, 1, 1),
-            (1, 0, 2), (0, 0, 3), (1, 1, 2),
-            (1, 0, 3), (0, 1, 3), (1, 1, 3),
-        ]
-        product_after = {7: 0, 10: 1, 13: 2}
-        experts_before = {1: (0, 1), 2: (1, 0), 4: (1, 1)}
-        for step, (pool, e, t) in enumerate(order):
-            if step in experts_before:
-                expert(*experts_before[step])
-            turn(pool, e, t)
-            scatter(pool, e, t)
-            if step in product_after:
-                product(nc.vector, product_after[step], slice(0, T))
+        last = PACK - 1
+        parts = [slice(u * PART, (u + 1) * PART) for u in range(T // PART)]
+        grouped = [held.tile([P, PART, PACK], BF16, name=f"grouped{u}", align_bytes=64) for u in range(len(parts))]
+        by_scalar = [0, 2, 3]
+        for u in by_scalar:
+            nc.scalar.copy(grouped[u][:, :, 0:last], planes[:, 0:last, parts[u]].rearrange("p t c -> p c t"))
+        put_back(1, both, 3)
 
-        halves = [slice(0, HALF), slice(HALF, T)]
-        product(nc.vector, PACK - 1, halves[1])
-        product(nc.vector, PACK - 1, halves[0])
-        grouped = []
-        for u in range(2):
-            tile = held.tile([P, HALF, PACK], BF16, name=f"grouped{u}", align_bytes=64)
-            dst = tile[:].rearrange("p (c i) t -> p c t i", i=4)
-            src = planes[:, :, halves[u]].rearrange("p t (c i) -> p c t i", i=4)
-            if u == 0:
-                nc.vector.tensor_copy(dst, src)
-            else:
-                nc.scalar.copy(dst, src)
-            grouped.append(tile)
-        for u in range(2):
-            h_words = held.tile([P, HALF], U32, name=f"h_words{u}", align_bytes=64)
-            h_scales = held.tile([P, HALF], U8, name=f"h_scales{u}", align_bytes=64)
+        product(nc.vector, last, parts[0])
+        product(nc.vector, last, parts[1])
+        product(nc.vector, last, slice(2 * PART, T))
+        for u in by_scalar:
+            nc.scalar.copy(grouped[u][:, :, last], planes[:, last, parts[u]])
+        nc.vector.tensor_copy(
+            grouped[1][:].rearrange("p (c i) t -> p c t i", i=4),
+            planes[:, :, parts[1]].rearrange("p t (c i) -> p c t i", i=4),
+        )
+        result = held.tile([N, T], F32, name="result")
+        for u in range(len(parts)):
+            h_words = held.tile([P, PART], U32, name=f"h_words{u}", align_bytes=64)
+            h_scales = held.tile([P, PART], U8, name=f"h_scales{u}", align_bytes=64)
             nc.vector.quantize_mx(
                 out=h_words[:].bitcast(FP8X4),
                 scales=h_scales[:],
                 in_=grouped[u][:].rearrange("p c t -> p (c t)"),
             )
-            total = ps_out.tile([N, HALF], F32, name=f"total{u}")
+            total = ps_out.tile([N, PART], F32, name=f"total{u}")
             nc.tensor.matmul_mx(
                 out=total[:],
                 lhsT=w2w[:].bitcast(FP8X4),
@@ -185,9 +191,10 @@ def tile_moe_pool_relu_kernel(tc, x_words, x_scales, wa_words, wa_scales, wb_wor
                 start=True,
                 stop=True,
             )
-            result = held.tile([N, HALF], F32, name=f"result{u}")
-            if u == 0:
-                nc.scalar.copy(result[:], total[:])
+            if u < 3:
+                nc.scalar.copy(result[:, parts[u]], total[:])
             else:
-                nc.vector.tensor_copy(result[:], total[:])
-            nc.sync.dma_start(out[:, halves[u]], result[:])
+                nc.vector.tensor_copy(result[:, parts[u]], total[:])
+            if u > 0:
+                cols = slice(0, 2 * PART) if u == 1 else parts[u]
+                nc.sync.dma_start(out[:, cols], result[:, cols])

@@ -45,7 +45,7 @@ def tile_moe_pool_relu_kernel(tc, x_words, x_scales, wa_words, wa_scales, wb_wor
 
         def zeroed_plane(name):
             tile = held.tile([P, H // 4], I32, name=name, align_bytes=64)
-            nc.gpsimd.memset(tile[:], 0)
+            nc.vector.memset(tile[:], 0)
             return tile
 
         def load_pool_scales(tile, dram, queues):
@@ -62,7 +62,7 @@ def tile_moe_pool_relu_kernel(tc, x_words, x_scales, wa_words, wa_scales, wb_wor
         xw = load_words("xw", x_words[0], T, nc.scalar)
         xs = load_scales_repeated("xs", x_scales[0], T, nc.sync)
         ww[0, 0] = load_words("wa0", wa_words[0, 0], H, nc.scalar)
-        load_pool_scales(pool_planes[0], wa_scales, [nc.gpsimd, nc.gpsimd, nc.gpsimd, nc.sync])
+        load_pool_scales(pool_planes[0], wa_scales, [nc.sync] * 4)
         nc.sync.dma_start(lists[1][:], offs2)
         ww[0, 1] = load_words("wa1", wa_words[1, 0], H, nc.sync)
         ww[1, 0] = load_words("wb0", wb_words[0, 0], H, nc.sync)

@@ -4,7 +4,7 @@ import concourse.mybir as mybir
 from concourse.masks import make_identity
 
 K, T, H, N = 512, 512, 512, 128
-E, C = 2, 256
+EXPERTS, SLOTS_PER_EXPERT = 2, 256
 FLOPS = 2 * (2 * K * H * T) + 2 * H * N * T
 
 F32 = mybir.dt.float32
@@ -19,182 +19,203 @@ MULT = mybir.AluOpType.mult
 
 P = 128
 PACK = 4
-WIDE = 704
-PART = 128
+LAST = PACK - 1
+QUADRANTS = 4
+POOL_A, POOL_C = 0, 1
+WINDOW = 704
+PARTS = [slice(0, 128), slice(128, 256), slice(256, 384), slice(384, 448), slice(448, 512)]
+PARTS_ON_VECTOR = [1, 3]
+BANKS = [[0, 1], [2], [3], [4]]
+STORES = {1: [0, 1], 2: [2], 4: [3, 4]}
 
 
-def tile_moe_pool_relu_kernel(tc, x_words, x_scales, wa_words, wa_scales, wb_words, wb_scales, w2_words, w2_scales, offs, offs2, out):
+def tile_moe_pool_relu_kernel(
+    tc, x_words, x_scales, wa_words, wa_scales, wb_words, wb_scales, w2_words, w2_scales, offs, offs2, out
+):
     nc = tc.nc
     with ExitStack() as ctx:
         held = ctx.enter_context(tc.tile_pool(name="held", bufs=1))
-        ps_mm = ctx.enter_context(tc.psum_pool(name="ps_mm", bufs=2))
-        ps_tr = ctx.enter_context(tc.psum_pool(name="ps_tr", bufs=2))
+        ps_sums = ctx.enter_context(tc.psum_pool(name="ps_sums", bufs=2))
+        ps_turned = ctx.enter_context(tc.psum_pool(name="ps_turned", bufs=2))
         ps_out = ctx.enter_context(tc.psum_pool(name="ps_out", bufs=1))
 
-        def load_words(name, dram, width, queue):
-            tile = held.tile([P, width], I32, name=name, align_bytes=64)
-            queue.dma_start(tile[:], dram.rearrange("p c d -> p (c d)").bitcast(I32))
+        def load_words(name, dram, queue, tile_width):
+            tile = held.tile([P, tile_width], I32, name=name, align_bytes=64)
+            queue.dma_start(tile[:, 0 : dram.shape[1]], dram.rearrange("p c d -> p (c d)").bitcast(I32))
             return tile
 
-        def load_scales_repeated(name, dram, width, queue):
-            tile = held.tile([P, width], U8, name=name, align_bytes=64)
-            for q in range(4):
-                rows = dram[4 * q : 4 * q + 4, :].bitcast(I32).unsqueeze(0)
-                queue.dma_start(tile[32 * q : 32 * q + 32, :].bitcast(I32), rows.to_broadcast([8, 4, width // 4]))
-            return tile
-
-        def zeroed_plane(name):
-            tile = held.tile([P, H // 4], I32, name=name, align_bytes=64)
-            nc.vector.memset(tile[:], 0)
-            return tile
-
-        def load_pool_scales(tile, dram, queues):
+        def load_scales_repeated(name, dram, queues, tile_width):
+            width = dram.shape[1]
+            tile = held.tile([P, tile_width], U8, name=name, align_bytes=64)
             for q, queue in enumerate(queues):
-                queue.dma_start(tile[32 * q : 32 * q + 4 * E, :], dram[:, 0, 4 * q : 4 * q + 4, :].bitcast(I32))
+                rows = dram[4 * q : 4 * q + 4, :].bitcast(I32).unsqueeze(0)
+                queue.dma_start(tile[32 * q : 32 * q + 32, 0:width].bitcast(I32), rows.to_broadcast([8, 4, width // 4]))
+            return tile
+
+        pool_scales = []
+        for pool in (POOL_A, POOL_C):
+            tile = held.tile([P, H // 4], I32, name=f"pool_scales{pool}", align_bytes=64)
+            nc.vector.memset(tile[:], 0)
+            pool_scales.append(tile)
+
+        def load_pool_scales(pool, dram):
+            for q in range(QUADRANTS):
+                nc.sync.dma_start(
+                    pool_scales[pool][32 * q : 32 * q + 4 * EXPERTS, :], dram[:, 0, 4 * q : 4 * q + 4, :].bitcast(I32)
+                )
 
         lists = [held.tile([P, T // 16], U16, name="list_a"), held.tile([P, T // 16], U16, name="list_c")]
-        ww, ws = {}, {}
-        pool_planes = [zeroed_plane("was"), zeroed_plane("wbs")]
-        for pool in range(2):
-            for e in range(E):
-                ws[pool, e] = pool_planes[pool][4 * e :, :].bitcast(U8)
-        nc.sync.dma_start(lists[0][:], offs)
-        xw = load_words("xw", x_words[0], T, nc.scalar)
-        xs = load_scales_repeated("xs", x_scales[0], T, nc.sync)
-        ww[0, 0] = load_words("wa0", wa_words[0, 0], H, nc.scalar)
-        load_pool_scales(pool_planes[0], wa_scales, [nc.sync] * 4)
-        nc.sync.dma_start(lists[1][:], offs2)
-        ww[0, 1] = load_words("wa1", wa_words[1, 0], H, nc.sync)
-        ww[1, 0] = load_words("wb0", wb_words[0, 0], H, nc.sync)
-        load_pool_scales(pool_planes[1], wb_scales, [nc.sync] * 4)
-        ww[1, 1] = load_words("wb1", wb_words[1, 0], H, nc.sync)
-        w2w = load_words("w2w", w2_words[0], N, nc.sync)
-        w2s = load_scales_repeated("w2s", w2_scales[0], N, nc.sync)
+        weights = {}
+        nc.sync.dma_start(lists[POOL_A][:], offs)
+        token_scales = load_scales_repeated("token_scales", x_scales[0], [nc.scalar, nc.sync, nc.scalar, nc.sync], WINDOW)
+        token_words = load_words("token_words", x_words[0], nc.scalar, WINDOW)
+        weights[POOL_A, 0] = load_words("wa0", wa_words[0, 0], nc.scalar, H)
+        load_pool_scales(POOL_A, wa_scales)
+        nc.sync.dma_start(lists[POOL_C][:], offs2)
+        weights[POOL_A, 1] = load_words("wa1", wa_words[1, 0], nc.sync, H)
+        weights[POOL_C, 0] = load_words("wb0", wb_words[0, 0], nc.sync, H)
+        load_pool_scales(POOL_C, wb_scales)
+        weights[POOL_C, 1] = load_words("wb1", wb_words[1, 0], nc.sync, H)
+        w2_codes = load_words("w2_codes", w2_words[0], nc.sync, N)
+        w2_plane = load_scales_repeated("w2_plane", w2_scales[0], [nc.sync] * QUADRANTS, N)
 
         identity = held.tile([P, P], F32, name="identity", align_bytes=64)
         make_identity(nc, identity[:])
 
-        def slots(pool, blocks):
+        def offsets(pool, blocks):
             return lists[pool][:, blocks[0] * (P // 16) : (blocks[-1] + 1) * (P // 16)]
 
-        gathered = {}
+        slot_words, slot_scales = {}, {}
 
-        def gather(pool, e):
-            words = held.tile([P, C], U32, name=f"g_words{pool}{e}", align_bytes=64)
-            scales = held.tile([P, C], U8, name=f"g_scales{pool}{e}", align_bytes=64)
-            nc.vector.tensor_copy(scales[:], xs[:].indirect(slots(pool, [2 * e, 2 * e + 1])))
-            nc.vector.tensor_copy(words[:], xw[:].bitcast(U32).indirect(slots(pool, [2 * e, 2 * e + 1])))
-            gathered[pool, e] = (words, scales)
-
-        rows = {}
-
-        def expert(pool, e):
-            words, scales = gathered[pool, e]
-            for b in range(C // P):
-                cols = slice(b * P, (b + 1) * P)
-                acc = ps_mm.tile([P, H], F32, name="acc")
-                nc.tensor.matmul_mx(
-                    out=acc[:],
-                    lhsT=words[:, cols].bitcast(FP8X4),
-                    lhsT_scale=scales[:, cols],
-                    rhs=ww[pool, e][:].bitcast(FP8X4),
-                    rhs_scale=ws[pool, e],
-                    start=True,
-                    stop=True,
-                )
-                row = held.tile([P, PACK, P], F32, name=f"row{pool}{e}{b}", align_bytes=64)
-                by_plane = acc[:].rearrange("s (p t) -> s t p", t=PACK)
-                if pool == 0:
-                    nc.scalar.activation(row[:], by_plane, RELU)
-                else:
-                    nc.scalar.copy(row[:], by_plane)
-                rows[pool, 2 * e + b] = row
-
-        windows = {}
-        for pool in range(2):
-            for t in range(PACK):
-                width = T if pool == 0 and t < 2 else WIDE
-                windows[pool, t] = held.tile([P, width], F32, name=f"window{pool}{t}", align_bytes=64)
-
-        def put_back(pool, blocks, t):
-            width = P * len(blocks)
-            bank = ps_tr.tile([P, width], F32, name="bank")
+        def gather(name, into, window, dtype, pool, blocks):
+            tile = held.tile([P, P * len(blocks)], dtype, name=f"{name}{pool}{blocks[0]}", align_bytes=64)
+            nc.vector.tensor_copy(tile[:], window[:].bitcast(dtype).indirect(offsets(pool, blocks)))
             for j, block in enumerate(blocks):
-                nc.tensor.transpose(bank[:, j * P : (j + 1) * P], rows[pool, block][:, t, :], identity[:])
-            src = held.tile([P, width], F32, name=f"src{pool}{blocks[0]}{t}", align_bytes=64)
-            nc.scalar.copy(src[:], bank[:])
-            nc.vector.tensor_copy(windows[pool, t][:].indirect(slots(pool, blocks)), src[:])
+                into[pool, block] = tile[:, j * P : (j + 1) * P]
 
-        planes = held.tile([P, PACK, T], BF16, name="planes", align_bytes=64)
+        sums, by_slot = {}, {}
 
-        def product(engine, t, cols):
-            engine.tensor_tensor(planes[:, t, cols], windows[0, t][:, cols], windows[1, t][:, cols], MULT)
-
-        both = [0, 1, 2, 3]
-        everyone = slice(0, T)
-        gather(0, 0)
-        expert(0, 0)
-        gather(0, 1)
-        gather(1, 0)
-        gather(1, 1)
-        put_back(0, [0], 0)
-        put_back(0, [0], 1)
-        put_back(0, [1], 0)
-        expert(0, 1)
-        put_back(0, [1], 1)
-        put_back(0, [2, 3], 0)
-        expert(1, 0)
-        put_back(0, [2, 3], 1)
-        expert(1, 1)
-        put_back(0, both, 2)
-        put_back(1, both, 0)
-        product(nc.gpsimd, 0, everyone)
-        put_back(1, both, 1)
-        product(nc.gpsimd, 1, everyone)
-        put_back(1, both, 2)
-        product(nc.gpsimd, 2, everyone)
-        put_back(0, both, 3)
-
-        last = PACK - 1
-        parts = [slice(u * PART, (u + 1) * PART) for u in range(T // PART)]
-        grouped = [held.tile([P, PART, PACK], BF16, name=f"grouped{u}", align_bytes=64) for u in range(len(parts))]
-        by_scalar = [0, 2, 3]
-        for u in by_scalar:
-            nc.scalar.copy(grouped[u][:, :, 0:last], planes[:, 0:last, parts[u]].rearrange("p t c -> p c t"))
-        put_back(1, both, 3)
-
-        product(nc.vector, last, parts[0])
-        product(nc.vector, last, parts[1])
-        product(nc.vector, last, slice(2 * PART, T))
-        for u in by_scalar:
-            nc.scalar.copy(grouped[u][:, :, last], planes[:, last, parts[u]])
-        nc.vector.tensor_copy(
-            grouped[1][:].rearrange("p (c i) t -> p c t i", i=4),
-            planes[:, :, parts[1]].rearrange("p t (c i) -> p c t i", i=4),
-        )
-        result = held.tile([N, T], F32, name="result")
-        for u in range(len(parts)):
-            h_words = held.tile([P, PART], U32, name=f"h_words{u}", align_bytes=64)
-            h_scales = held.tile([P, PART], U8, name=f"h_scales{u}", align_bytes=64)
-            nc.vector.quantize_mx(
-                out=h_words[:].bitcast(FP8X4),
-                scales=h_scales[:],
-                in_=grouped[u][:].rearrange("p c t -> p (c t)"),
-            )
-            total = ps_out.tile([N, PART], F32, name=f"total{u}")
+        def multiply(pool, block):
+            e = block * P // SLOTS_PER_EXPERT
+            acc = ps_sums.tile([P, H], F32, name="acc")
             nc.tensor.matmul_mx(
-                out=total[:],
-                lhsT=w2w[:].bitcast(FP8X4),
-                lhsT_scale=w2s[:],
-                rhs=h_words[:].bitcast(FP8X4),
-                rhs_scale=h_scales[:],
+                out=acc[:],
+                lhsT=slot_words[pool, block].bitcast(FP8X4),
+                lhsT_scale=slot_scales[pool, block],
+                rhs=weights[pool, e][:].bitcast(FP8X4),
+                rhs_scale=pool_scales[pool][4 * e :, :].bitcast(U8),
                 start=True,
                 stop=True,
             )
-            if u < 3:
-                nc.scalar.copy(result[:, parts[u]], total[:])
+            sums[pool, block] = acc[:].rearrange("s (p t) -> s t p", t=PACK)
+            by_slot[pool, block] = held.tile([P, PACK, P], F32, name=f"by_slot{pool}{block}", align_bytes=64)
+
+        def empty(pool, block, first_plane, stop_plane):
+            dst = by_slot[pool, block][:, first_plane:stop_plane, :]
+            src = sums[pool, block][:, first_plane:stop_plane, :]
+            if pool == POOL_A:
+                nc.scalar.activation(dst, src, RELU)
             else:
-                nc.vector.tensor_copy(result[:, parts[u]], total[:])
-            if u > 0:
-                cols = slice(0, 2 * PART) if u == 1 else parts[u]
-                nc.sync.dma_start(out[:, cols], result[:, cols])
+                nc.scalar.copy(dst, src)
+
+        def multiply_and_empty(pool, blocks):
+            for block in blocks:
+                multiply(pool, block)
+                empty(pool, block, 0, PACK)
+
+        by_token = {}
+        for pool in (POOL_A, POOL_C):
+            for t in range(PACK):
+                by_token[pool, t] = held.tile([P, WINDOW], F32, name=f"by_token{pool}{t}", align_bytes=64)
+
+        def put_back(pool, blocks, t):
+            width = P * len(blocks)
+            turned = ps_turned.tile([P, width], F32, name="turned")
+            for j, block in enumerate(blocks):
+                nc.tensor.transpose(turned[:, j * P : (j + 1) * P], by_slot[pool, block][:, t, :], identity[:])
+            staged = held.tile([P, width], F32, name=f"staged{pool}{blocks[0]}{t}", align_bytes=64)
+            nc.scalar.copy(staged[:], turned[:])
+            nc.vector.tensor_copy(by_token[pool, t][:].indirect(offsets(pool, blocks)), staged[:])
+
+        h_planes = held.tile([P, PACK, T], BF16, name="h_planes", align_bytes=64)
+
+        def product(engine, t, tokens):
+            engine.tensor_tensor(h_planes[:, t, tokens], by_token[POOL_A, t][:, tokens], by_token[POOL_C, t][:, tokens], MULT)
+
+        all_blocks = [0, 1, 2, 3]
+        all_tokens = slice(0, T)
+
+        gather("slot_scales", slot_scales, token_scales, U8, POOL_A, [0, 1])
+        gather("slot_words", slot_words, token_words, U32, POOL_A, [0, 1])
+        multiply(POOL_A, 0)
+        empty(POOL_A, 0, 0, 1)
+        gather("slot_scales", slot_scales, token_scales, U8, POOL_A, [2, 3])
+        gather("slot_words", slot_words, token_words, U32, POOL_A, [2, 3])
+        gather("slot_scales", slot_scales, token_scales, U8, POOL_C, all_blocks)
+        gather("slot_words", slot_words, token_words, U32, POOL_C, all_blocks)
+        put_back(POOL_A, [0], 0)
+        empty(POOL_A, 0, 1, PACK)
+        put_back(POOL_A, [0], 1)
+        multiply_and_empty(POOL_A, [1])
+        put_back(POOL_A, [1], 0)
+        multiply_and_empty(POOL_A, [2, 3])
+        put_back(POOL_A, [1], 1)
+        put_back(POOL_A, [2, 3], 0)
+        multiply_and_empty(POOL_C, [0, 1])
+        put_back(POOL_A, [2, 3], 1)
+        multiply_and_empty(POOL_C, [2, 3])
+        put_back(POOL_A, all_blocks, 2)
+        for t in range(LAST):
+            put_back(POOL_C, all_blocks, t)
+            product(nc.gpsimd, t, all_tokens)
+        put_back(POOL_A, all_blocks, LAST)
+
+        side_by_side = []
+        for u, part in enumerate(PARTS):
+            tile = held.tile([P, part.stop - part.start, PACK], BF16, name=f"side_by_side{u}", align_bytes=64)
+            side_by_side.append(tile)
+        parts_on_scalar = [u for u in range(len(PARTS)) if u not in PARTS_ON_VECTOR]
+        for u in parts_on_scalar:
+            nc.scalar.copy(side_by_side[u][:, :, 0:LAST], h_planes[:, 0:LAST, PARTS[u]].rearrange("p t c -> p c t"))
+        put_back(POOL_C, all_blocks, LAST)
+
+        for tokens in (PARTS[0], slice(PARTS[1].start, PARTS[2].stop), slice(PARTS[3].start, T)):
+            product(nc.vector, LAST, tokens)
+        for u in parts_on_scalar:
+            nc.scalar.copy(side_by_side[u][:, :, LAST], h_planes[:, LAST, PARTS[u]])
+        for u in PARTS_ON_VECTOR:
+            nc.vector.tensor_copy(
+                side_by_side[u][:].rearrange("p (c i) t -> p c t i", i=4),
+                h_planes[:, :, PARTS[u]].rearrange("p t (c i) -> p c t i", i=4),
+            )
+
+        result = held.tile([N, T], F32, name="result")
+        for b, bank_parts in enumerate(BANKS):
+            tokens = slice(PARTS[bank_parts[0]].start, PARTS[bank_parts[-1]].stop)
+            total = ps_out.tile([N, tokens.stop - tokens.start], F32, name=f"total{b}")
+            for u in bank_parts:
+                width = PARTS[u].stop - PARTS[u].start
+                h_words = held.tile([P, width], U32, name=f"h_words{u}", align_bytes=64)
+                h_scales = held.tile([P, width], U8, name=f"h_scales{u}", align_bytes=64)
+                nc.vector.quantize_mx(
+                    out=h_words[:].bitcast(FP8X4),
+                    scales=h_scales[:],
+                    in_=side_by_side[u][:].rearrange("p c t -> p (c t)"),
+                )
+                nc.tensor.matmul_mx(
+                    out=total[:, PARTS[u].start - tokens.start : PARTS[u].stop - tokens.start],
+                    lhsT=w2_codes[:].bitcast(FP8X4),
+                    lhsT_scale=w2_plane[:],
+                    rhs=h_words[:].bitcast(FP8X4),
+                    rhs_scale=h_scales[:],
+                    start=True,
+                    stop=True,
+                )
+            if b < len(BANKS) - 1:
+                nc.scalar.copy(result[:, tokens], total[:])
+            else:
+                nc.vector.tensor_copy(result[:, tokens], total[:])
+            if bank_parts[-1] in STORES:
+                stored = STORES[bank_parts[-1]]
+                columns = slice(PARTS[stored[0]].start, PARTS[stored[-1]].stop)
+                nc.sync.dma_start(out[:, columns], result[:, columns])

@@ -23,10 +23,11 @@ LAST = PACK - 1
 QUADRANTS = 4
 POOL_A, POOL_C = 0, 1
 WINDOW = 704
-PARTS = [slice(0, 128), slice(128, 256), slice(256, 384), slice(384, 448), slice(448, 512)]
-PARTS_ON_VECTOR = [1, 3]
-BANKS = [[0, 1], [2], [3], [4]]
-STORES = {1: [0, 1], 2: [2], 4: [3, 4]}
+PARTS = [slice(0, 128), slice(128, 256), slice(256, 320), slice(320, 448), slice(448, 512)]
+PARTS_ON_SCALAR = [0, 1, 2]
+PARTS_ON_VECTOR = [3, 4]
+BANKS = [[0], [3, 4], [1], [2]]
+STORES = {0: [0], 4: [3, 4], 2: [1, 2]}
 
 
 def tile_moe_pool_relu_kernel(
@@ -124,9 +125,15 @@ def tile_moe_pool_relu_kernel(
                 empty(pool, block, 0, PACK)
 
         by_token = {}
+
+        def open_window(pool, t):
+            tag = f"by_token{pool}{min(t, LAST - 1) if pool == POOL_C else t}"
+            by_token[pool, t] = held.tile([P, WINDOW], F32, name=f"by_token{pool}{t}", tag=tag, align_bytes=64)
+
         for pool in (POOL_A, POOL_C):
             for t in range(PACK):
-                by_token[pool, t] = held.tile([P, WINDOW], F32, name=f"by_token{pool}{t}", align_bytes=64)
+                if (pool, t) != (POOL_C, LAST):
+                    open_window(pool, t)
 
         def put_back(pool, blocks, t):
             width = P * len(blocks)
@@ -137,13 +144,15 @@ def tile_moe_pool_relu_kernel(
             nc.scalar.copy(staged[:], turned[:])
             nc.vector.tensor_copy(by_token[pool, t][:].indirect(offsets(pool, blocks)), staged[:])
 
-        h_planes = held.tile([P, PACK, T], BF16, name="h_planes", align_bytes=64)
+        side_by_side = []
+        for u, part in enumerate(PARTS):
+            tile = held.tile([P, part.stop - part.start, PACK], BF16, name=f"side_by_side{u}", align_bytes=64)
+            side_by_side.append(tile)
 
-        def product(engine, t, tokens):
-            engine.tensor_tensor(h_planes[:, t, tokens], by_token[POOL_A, t][:, tokens], by_token[POOL_C, t][:, tokens], MULT)
+        def product(engine, dst, t, tokens):
+            engine.tensor_tensor(dst, by_token[POOL_A, t][:, tokens], by_token[POOL_C, t][:, tokens], MULT)
 
         all_blocks = [0, 1, 2, 3]
-        all_tokens = slice(0, T)
 
         gather("slot_scales", slot_scales, token_scales, U8, POOL_A, [0, 1])
         gather("slot_words", slot_words, token_words, U32, POOL_A, [0, 1])
@@ -167,27 +176,20 @@ def tile_moe_pool_relu_kernel(
         put_back(POOL_A, all_blocks, 2)
         for t in range(LAST):
             put_back(POOL_C, all_blocks, t)
-            product(nc.gpsimd, t, all_tokens)
+            for u, part in enumerate(PARTS):
+                product(nc.gpsimd, side_by_side[u][:, :, t], t, part)
         put_back(POOL_A, all_blocks, LAST)
 
-        side_by_side = []
-        for u, part in enumerate(PARTS):
-            tile = held.tile([P, part.stop - part.start, PACK], BF16, name=f"side_by_side{u}", align_bytes=64)
-            side_by_side.append(tile)
-        parts_on_scalar = [u for u in range(len(PARTS)) if u not in PARTS_ON_VECTOR]
-        for u in parts_on_scalar:
-            nc.scalar.copy(side_by_side[u][:, :, 0:LAST], h_planes[:, 0:LAST, PARTS[u]].rearrange("p t c -> p c t"))
+        open_window(POOL_C, LAST)
         put_back(POOL_C, all_blocks, LAST)
 
-        for tokens in (PARTS[0], slice(PARTS[1].start, PARTS[2].stop), slice(PARTS[3].start, T)):
-            product(nc.vector, LAST, tokens)
-        for u in parts_on_scalar:
-            nc.scalar.copy(side_by_side[u][:, :, LAST], h_planes[:, LAST, PARTS[u]])
+        last_plane = held.tile([P, T], BF16, name="last_plane", align_bytes=64)
+        for tokens in (PARTS[0], slice(PARTS[1].start, PARTS[2].stop)):
+            product(nc.vector, last_plane[:, tokens], LAST, tokens)
+        for u in PARTS_ON_SCALAR:
+            nc.scalar.copy(side_by_side[u][:, :, LAST], last_plane[:, PARTS[u]])
         for u in PARTS_ON_VECTOR:
-            nc.vector.tensor_copy(
-                side_by_side[u][:].rearrange("p (c i) t -> p c t i", i=4),
-                h_planes[:, :, PARTS[u]].rearrange("p t (c i) -> p c t i", i=4),
-            )
+            product(nc.vector, side_by_side[u][:, :, LAST], LAST, PARTS[u])
 
         result = held.tile([N, T], F32, name="result")
         for b, bank_parts in enumerate(BANKS):

@@ -1,7 +1,6 @@
 from contextlib import ExitStack
 
 import concourse.mybir as mybir
-from concourse.masks import make_identity
 
 K, T, H, N = 512, 512, 512, 128
 EXPERTS, SLOTS_PER_EXPERT = 2, 256
@@ -36,8 +35,8 @@ def tile_moe_pool_relu_kernel(
     nc = tc.nc
     with ExitStack() as ctx:
         held = ctx.enter_context(tc.tile_pool(name="held", bufs=1))
-        ps_sums = ctx.enter_context(tc.psum_pool(name="ps_sums", bufs=2))
-        ps_turned = ctx.enter_context(tc.psum_pool(name="ps_turned", bufs=2))
+        ps_sums = ctx.enter_context(tc.psum_pool(name="ps_sums", bufs=1))
+        uses = []
         ps_out = ctx.enter_context(tc.psum_pool(name="ps_out", bufs=1))
 
         def load_words(name, dram, queue, tile_width):
@@ -80,49 +79,42 @@ def tile_moe_pool_relu_kernel(
         w2_codes = load_words("w2_codes", w2_words[0], nc.sync, N)
         w2_plane = load_scales_repeated("w2_plane", w2_scales[0], [nc.sync] * QUADRANTS, N)
 
-        identity = held.tile([P, P], F32, name="identity", align_bytes=64)
-        make_identity(nc, identity[:])
+        sorted_words, sorted_scales = {}, {}
 
-        def offsets(pool, blocks):
-            return lists[pool][:, blocks[0] * (P // 16) : (blocks[-1] + 1) * (P // 16)]
+        def sort_columns(into, key, source, dtype, name, plane_runs):
+            by_plane = source.rearrange("k (p t) -> k t p", t=PACK)
+            for planes in plane_runs:
+                tile = held.tile([P, len(planes), P], dtype, name=f"{name}{planes[0]}", align_bytes=64)
+                nc.gpsimd.tensor_copy(tile[:], by_plane[:, planes[0] : planes[-1] + 1, :])
+                for n, t in enumerate(planes):
+                    into[key, t] = tile[:, n, :]
 
+        def sort_words(pool, e, plane_runs):
+            sort_columns(sorted_words, (pool, e), weights[pool, e][:].bitcast(U32), U32, f"sorted_w{pool}{e}", plane_runs)
+
+        def sort_scales(pool, plane_runs):
+            sort_columns(sorted_scales, pool, pool_scales[pool][:].bitcast(U8), U8, f"sorted_s{pool}", plane_runs)
+
+        sort_words(POOL_A, 0, [[0], [1]])
+        sort_scales(POOL_A, [[0], [1]])
+        sort_words(POOL_A, 1, [[1], [0]])
+        sort_scales(POOL_A, [[2, 3]])
+        sort_words(POOL_A, 0, [[2, 3]])
+        sort_words(POOL_A, 1, [[2, 3]])
+        sort_words(POOL_C, 0, [[0, 1, 2, 3]])
+        sort_words(POOL_C, 1, [[0, 1, 2, 3]])
+        sort_scales(POOL_C, [[0, 1, 2, 3]])
+
+        def offsets(pool, experts):
+            return lists[pool][:, experts[0] * (SLOTS_PER_EXPERT // 16) : (experts[-1] + 1) * (SLOTS_PER_EXPERT // 16)]
+
+        both = [0, 1]
         slot_words, slot_scales = {}, {}
-
-        def gather(name, into, window, dtype, pool, blocks):
-            tile = held.tile([P, P * len(blocks)], dtype, name=f"{name}{pool}{blocks[0]}", align_bytes=64)
-            nc.vector.tensor_copy(tile[:], window[:].bitcast(dtype).indirect(offsets(pool, blocks)))
-            for j, block in enumerate(blocks):
-                into[pool, block] = tile[:, j * P : (j + 1) * P]
-
-        sums, by_slot = {}, {}
-
-        def multiply(pool, block):
-            e = block * P // SLOTS_PER_EXPERT
-            acc = ps_sums.tile([P, H], F32, name="acc")
-            nc.tensor.matmul_mx(
-                out=acc[:],
-                lhsT=slot_words[pool, block].bitcast(FP8X4),
-                lhsT_scale=slot_scales[pool, block],
-                rhs=weights[pool, e][:].bitcast(FP8X4),
-                rhs_scale=pool_scales[pool][4 * e :, :].bitcast(U8),
-                start=True,
-                stop=True,
-            )
-            sums[pool, block] = acc[:].rearrange("s (p t) -> s t p", t=PACK)
-            by_slot[pool, block] = held.tile([P, PACK, P], F32, name=f"by_slot{pool}{block}", align_bytes=64)
-
-        def empty(pool, block, first_plane, stop_plane):
-            dst = by_slot[pool, block][:, first_plane:stop_plane, :]
-            src = sums[pool, block][:, first_plane:stop_plane, :]
-            if pool == POOL_A:
-                nc.scalar.activation(dst, src, RELU)
-            else:
-                nc.scalar.copy(dst, src)
-
-        def multiply_and_empty(pool, blocks):
-            for block in blocks:
-                multiply(pool, block)
-                empty(pool, block, 0, PACK)
+        for pool in (POOL_A, POOL_C):
+            slot_scales[pool] = held.tile([P, T], U8, name=f"slot_scales{pool}", align_bytes=64)
+            slot_words[pool] = held.tile([P, T], U32, name=f"slot_words{pool}", align_bytes=64)
+            nc.vector.tensor_copy(slot_scales[pool][:], token_scales[:].indirect(offsets(pool, both)))
+            nc.vector.tensor_copy(slot_words[pool][:], token_words[:].bitcast(U32).indirect(offsets(pool, both)))
 
         by_token = {}
 
@@ -135,14 +127,27 @@ def tile_moe_pool_relu_kernel(
                 if (pool, t) != (POOL_C, LAST):
                     open_window(pool, t)
 
-        def put_back(pool, blocks, t):
-            width = P * len(blocks)
-            turned = ps_turned.tile([P, width], F32, name="turned")
-            for j, block in enumerate(blocks):
-                nc.tensor.transpose(turned[:, j * P : (j + 1) * P], by_slot[pool, block][:, t, :], identity[:])
-            staged = held.tile([P, width], F32, name=f"staged{pool}{blocks[0]}{t}", align_bytes=64)
-            nc.scalar.copy(staged[:], turned[:])
-            nc.vector.tensor_copy(by_token[pool, t][:].indirect(offsets(pool, blocks)), staged[:])
+        def put_back(pool, experts, t):
+            width = SLOTS_PER_EXPERT * len(experts)
+            uses.append(len(uses) % 2)
+            acc = ps_sums.tile([P, T], F32, name="acc", tag=f"acc{uses[-1]}")
+            for j, e in enumerate(experts):
+                slots = slice(e * SLOTS_PER_EXPERT, (e + 1) * SLOTS_PER_EXPERT)
+                nc.tensor.matmul_mx(
+                    out=acc[:, j * SLOTS_PER_EXPERT : (j + 1) * SLOTS_PER_EXPERT],
+                    lhsT=sorted_words[(pool, e), t].bitcast(FP8X4),
+                    lhsT_scale=sorted_scales[pool, t][4 * e :, :],
+                    rhs=slot_words[pool][:, slots].bitcast(FP8X4),
+                    rhs_scale=slot_scales[pool][:, slots],
+                    start=True,
+                    stop=True,
+                )
+            staged = held.tile([P, width], F32, name=f"staged{pool}{experts[0]}{t}", align_bytes=64)
+            if pool == POOL_A:
+                nc.scalar.activation(staged[:], acc[:, 0:width], RELU)
+            else:
+                nc.scalar.copy(staged[:], acc[:, 0:width])
+            nc.vector.tensor_copy(by_token[pool, t][:].indirect(offsets(pool, experts)), staged[:])
 
         side_by_side = []
         for u, part in enumerate(PARTS):
@@ -152,36 +157,18 @@ def tile_moe_pool_relu_kernel(
         def product(engine, dst, t, tokens):
             engine.tensor_tensor(dst, by_token[POOL_A, t][:, tokens], by_token[POOL_C, t][:, tokens], MULT)
 
-        all_blocks = [0, 1, 2, 3]
-
-        gather("slot_scales", slot_scales, token_scales, U8, POOL_A, [0, 1])
-        gather("slot_words", slot_words, token_words, U32, POOL_A, [0, 1])
-        multiply(POOL_A, 0)
-        empty(POOL_A, 0, 0, 1)
-        gather("slot_scales", slot_scales, token_scales, U8, POOL_A, [2, 3])
-        gather("slot_words", slot_words, token_words, U32, POOL_A, [2, 3])
-        gather("slot_scales", slot_scales, token_scales, U8, POOL_C, all_blocks)
-        gather("slot_words", slot_words, token_words, U32, POOL_C, all_blocks)
         put_back(POOL_A, [0], 0)
-        empty(POOL_A, 0, 1, PACK)
-        put_back(POOL_A, [0], 1)
-        multiply_and_empty(POOL_A, [1])
+        put_back(POOL_A, both, 1)
         put_back(POOL_A, [1], 0)
-        multiply_and_empty(POOL_A, [2, 3])
-        put_back(POOL_A, [1], 1)
-        put_back(POOL_A, [2, 3], 0)
-        multiply_and_empty(POOL_C, [0, 1])
-        put_back(POOL_A, [2, 3], 1)
-        multiply_and_empty(POOL_C, [2, 3])
-        put_back(POOL_A, all_blocks, 2)
+        put_back(POOL_A, both, 2)
         for t in range(LAST):
-            put_back(POOL_C, all_blocks, t)
+            put_back(POOL_C, both, t)
             for u, part in enumerate(PARTS):
                 product(nc.gpsimd, side_by_side[u][:, :, t], t, part)
-        put_back(POOL_A, all_blocks, LAST)
+        put_back(POOL_A, both, LAST)
 
         open_window(POOL_C, LAST)
-        put_back(POOL_C, all_blocks, LAST)
+        put_back(POOL_C, both, LAST)
 
         last_plane = held.tile([P, T], BF16, name="last_plane", align_bytes=64)
         for tokens in (PARTS[0], slice(PARTS[1].start, PARTS[2].stop)):

@@ -55,7 +55,7 @@ def tile_moe_pool_relu_kernel(
         pool_scales = []
         for pool in (POOL_A, POOL_C):
             tile = held.tile([P, H // 4], I32, name=f"pool_scales{pool}", align_bytes=64)
-            nc.vector.memset(tile[:], 0)
+            nc.gpsimd.memset(tile[:], 0)
             pool_scales.append(tile)
 
         def load_pool_scales(pool, dram):
@@ -70,8 +70,8 @@ def tile_moe_pool_relu_kernel(
         token_scales = load_scales_repeated("token_scales", x_scales[0], [nc.scalar, nc.sync, nc.scalar, nc.sync], WINDOW)
         token_words = load_words("token_words", x_words[0], nc.scalar, WINDOW)
         weights[POOL_A, 0] = load_words("wa0", wa_words[0, 0], nc.scalar, H)
-        load_pool_scales(POOL_A, wa_scales)
         nc.sync.dma_start(lists[POOL_C][:], offs2)
+        load_pool_scales(POOL_A, wa_scales)
         weights[POOL_A, 1] = load_words("wa1", wa_words[1, 0], nc.sync, H)
         weights[POOL_C, 0] = load_words("wb0", wb_words[0, 0], nc.sync, H)
         load_pool_scales(POOL_C, wb_scales)

@@ -22,6 +22,7 @@ LAST = PACK - 1
 QUADRANTS = 4
 POOL_A, POOL_C = 0, 1
 WINDOW = 704
+FIRST_SLOTS = 128
 PARTS = [slice(0, 128), slice(128, 256), slice(256, 320), slice(320, 448), slice(448, 512)]
 PARTS_ON_SCALAR = [0, 1, 2]
 PARTS_ON_VECTOR = [3, 4]
@@ -36,12 +37,14 @@ def tile_moe_pool_relu_kernel(
     with ExitStack() as ctx:
         held = ctx.enter_context(tc.tile_pool(name="held", bufs=1))
         ps_sums = ctx.enter_context(tc.psum_pool(name="ps_sums", bufs=1))
-        uses = []
         ps_out = ctx.enter_context(tc.psum_pool(name="ps_out", bufs=1))
+
+        def as_words(dram):
+            return dram.rearrange("p c d -> p (c d)").bitcast(I32)
 
         def load_words(name, dram, queue, tile_width):
             tile = held.tile([P, tile_width], I32, name=name, align_bytes=64)
-            queue.dma_start(tile[:, 0 : dram.shape[1]], dram.rearrange("p c d -> p (c d)").bitcast(I32))
+            queue.dma_start(tile[:, 0 : dram.shape[1]], as_words(dram))
             return tile
 
         def load_scales_repeated(name, dram, queues, tile_width):
@@ -65,89 +68,93 @@ def tile_moe_pool_relu_kernel(
                 )
 
         lists = [held.tile([P, T // 16], U16, name="list_a"), held.tile([P, T // 16], U16, name="list_c")]
-        weights = {}
         nc.sync.dma_start(lists[POOL_A][:], offs)
         token_scales = load_scales_repeated("token_scales", x_scales[0], [nc.scalar, nc.sync, nc.scalar, nc.sync], WINDOW)
         token_words = load_words("token_words", x_words[0], nc.scalar, WINDOW)
-        weights[POOL_A, 0] = load_words("wa0", wa_words[0, 0], nc.scalar, H)
+        wa_codes = held.tile([P, EXPERTS, H], I32, name="wa_codes", align_bytes=64)
+        nc.scalar.dma_start(wa_codes[:, 0, :], as_words(wa_words[0, 0]))
         nc.sync.dma_start(lists[POOL_C][:], offs2)
         load_pool_scales(POOL_A, wa_scales)
-        weights[POOL_A, 1] = load_words("wa1", wa_words[1, 0], nc.sync, H)
-        weights[POOL_C, 0] = load_words("wb0", wb_words[0, 0], nc.sync, H)
+        nc.sync.dma_start(wa_codes[:, 1, :], as_words(wa_words[1, 0]))
+        wb0_codes = load_words("wb0_codes", wb_words[0, 0], nc.sync, H)
         load_pool_scales(POOL_C, wb_scales)
-        weights[POOL_C, 1] = load_words("wb1", wb_words[1, 0], nc.sync, H)
+        wb1_codes = load_words("wb1_codes", wb_words[1, 0], nc.sync, H)
         w2_codes = load_words("w2_codes", w2_words[0], nc.sync, N)
-        w2_plane = load_scales_repeated("w2_plane", w2_scales[0], [nc.sync] * QUADRANTS, N)
+        w2_scale_tile = load_scales_repeated("w2_scale_tile", w2_scales[0], [nc.sync] * QUADRANTS, N)
 
-        sorted_words, sorted_scales = {}, {}
+        def sort_columns(into, name, source, dtype, planes):
+            tile = held.tile([P, len(planes), P], dtype, name=f"{name}_{planes[0]}", align_bytes=64)
+            by_plane = source.bitcast(dtype).rearrange("k (p t) -> k t p", t=PACK)
+            nc.gpsimd.tensor_copy(tile[:], by_plane[:, planes[0] : planes[-1] + 1, :])
+            for n, t in enumerate(planes):
+                into[t] = tile[:, n, :]
 
-        def sort_columns(into, key, source, dtype, name, plane_runs):
-            by_plane = source.rearrange("k (p t) -> k t p", t=PACK)
-            for planes in plane_runs:
-                tile = held.tile([P, len(planes), P], dtype, name=f"{name}{planes[0]}", align_bytes=64)
-                nc.gpsimd.tensor_copy(tile[:], by_plane[:, planes[0] : planes[-1] + 1, :])
-                for n, t in enumerate(planes):
-                    into[key, t] = tile[:, n, :]
+        sorted_words = {(pool, e): {} for pool in (POOL_A, POOL_C) for e in range(EXPERTS)}
+        sorted_scales = {POOL_A: {}, POOL_C: {}}
 
-        def sort_words(pool, e, plane_runs):
-            sort_columns(sorted_words, (pool, e), weights[pool, e][:].bitcast(U32), U32, f"sorted_w{pool}{e}", plane_runs)
+        early, late = [0, 1], [2, 3]
+        for t in early:
+            sort_columns(sorted_words[POOL_A, 0], "sorted_wa0", wa_codes[:, 0, :], U32, [t])
+        for t in early:
+            sort_columns(sorted_scales[POOL_A], "sorted_sa", pool_scales[POOL_A][:], U8, [t])
+        for t in early:
+            sort_columns(sorted_words[POOL_A, 1], "sorted_wa1", wa_codes[:, 1, :], U32, [t])
+        sort_columns(sorted_scales[POOL_A], "sorted_sa", pool_scales[POOL_A][:], U8, late)
+        wa_late = held.tile([P, EXPERTS, len(late), P], U32, name="wa_late", align_bytes=64)
+        wa_by_plane = wa_codes[:].bitcast(U32).rearrange("k e (p t) -> k e t p", t=PACK)
+        nc.gpsimd.tensor_copy(wa_late[:], wa_by_plane[:, :, late[0] : PACK, :])
+        for e in range(EXPERTS):
+            for n, t in enumerate(late):
+                sorted_words[POOL_A, e][t] = wa_late[:, e, n, :]
+        sort_columns(sorted_words[POOL_C, 0], "sorted_wb0", wb0_codes[:], U32, early + late)
+        sort_columns(sorted_words[POOL_C, 1], "sorted_wb1", wb1_codes[:], U32, early + late)
+        sort_columns(sorted_scales[POOL_C], "sorted_sb", pool_scales[POOL_C][:], U8, early + late)
 
-        def sort_scales(pool, plane_runs):
-            sort_columns(sorted_scales, pool, pool_scales[pool][:].bitcast(U8), U8, f"sorted_s{pool}", plane_runs)
+        def offsets(pool, slots):
+            return lists[pool][:, slots.start // 16 : slots.stop // 16]
 
-        sort_words(POOL_A, 0, [[0], [1]])
-        sort_scales(POOL_A, [[0], [1]])
-        sort_words(POOL_A, 1, [[1], [0]])
-        sort_scales(POOL_A, [[2, 3]])
-        sort_words(POOL_A, 0, [[2, 3]])
-        sort_words(POOL_A, 1, [[2, 3]])
-        sort_words(POOL_C, 0, [[0, 1, 2, 3]])
-        sort_words(POOL_C, 1, [[0, 1, 2, 3]])
-        sort_scales(POOL_C, [[0, 1, 2, 3]])
-
-        def offsets(pool, experts):
-            return lists[pool][:, experts[0] * (SLOTS_PER_EXPERT // 16) : (experts[-1] + 1) * (SLOTS_PER_EXPERT // 16)]
-
-        both = [0, 1]
+        all_slots = slice(0, T)
         slot_words, slot_scales = {}, {}
         for pool in (POOL_A, POOL_C):
             slot_scales[pool] = held.tile([P, T], U8, name=f"slot_scales{pool}", align_bytes=64)
             slot_words[pool] = held.tile([P, T], U32, name=f"slot_words{pool}", align_bytes=64)
-            nc.vector.tensor_copy(slot_scales[pool][:], token_scales[:].indirect(offsets(pool, both)))
-            nc.vector.tensor_copy(slot_words[pool][:], token_words[:].bitcast(U32).indirect(offsets(pool, both)))
+            nc.vector.tensor_copy(slot_scales[pool][:], token_scales[:].indirect(offsets(pool, all_slots)))
+            nc.vector.tensor_copy(slot_words[pool][:], token_words[:].bitcast(U32).indirect(offsets(pool, all_slots)))
 
         by_token = {}
 
-        def open_window(pool, t):
-            tag = f"by_token{pool}{min(t, LAST - 1) if pool == POOL_C else t}"
+        def open_window(pool, t, tag):
             by_token[pool, t] = held.tile([P, WINDOW], F32, name=f"by_token{pool}{t}", tag=tag, align_bytes=64)
 
-        for pool in (POOL_A, POOL_C):
-            for t in range(PACK):
-                if (pool, t) != (POOL_C, LAST):
-                    open_window(pool, t)
+        for t in range(PACK):
+            open_window(POOL_A, t, f"window_a{t}")
+        for t in range(LAST):
+            open_window(POOL_C, t, f"window_c{t}")
 
-        def put_back(pool, experts, t):
-            width = SLOTS_PER_EXPERT * len(experts)
-            uses.append(len(uses) % 2)
-            acc = ps_sums.tile([P, T], F32, name="acc", tag=f"acc{uses[-1]}")
-            for j, e in enumerate(experts):
-                slots = slice(e * SLOTS_PER_EXPERT, (e + 1) * SLOTS_PER_EXPERT)
-                nc.tensor.matmul_mx(
-                    out=acc[:, j * SLOTS_PER_EXPERT : (j + 1) * SLOTS_PER_EXPERT],
-                    lhsT=sorted_words[(pool, e), t].bitcast(FP8X4),
-                    lhsT_scale=sorted_scales[pool, t][4 * e :, :],
-                    rhs=slot_words[pool][:, slots].bitcast(FP8X4),
-                    rhs_scale=slot_scales[pool][:, slots],
-                    start=True,
-                    stop=True,
-                )
-            staged = held.tile([P, width], F32, name=f"staged{pool}{experts[0]}{t}", align_bytes=64)
+        put_back_so_far = []
+
+        def put_back(pool, slots, t):
+            width = slots.stop - slots.start
+            acc = ps_sums.tile([P, T], F32, name="acc", tag=f"acc{len(put_back_so_far) % 2}")
+            put_back_so_far.append((pool, slots, t))
+            for e in range(EXPERTS):
+                first, stop = max(slots.start, e * SLOTS_PER_EXPERT), min(slots.stop, (e + 1) * SLOTS_PER_EXPERT)
+                if first < stop:
+                    nc.tensor.matmul_mx(
+                        out=acc[:, first - slots.start : stop - slots.start],
+                        lhsT=sorted_words[pool, e][t].bitcast(FP8X4),
+                        lhsT_scale=sorted_scales[pool][t][4 * e :, :],
+                        rhs=slot_words[pool][:, first:stop].bitcast(FP8X4),
+                        rhs_scale=slot_scales[pool][:, first:stop],
+                        start=True,
+                        stop=True,
+                    )
+            staged = held.tile([P, width], F32, name=f"staged{pool}_{slots.start}_{t}", align_bytes=64)
             if pool == POOL_A:
                 nc.scalar.activation(staged[:], acc[:, 0:width], RELU)
             else:
                 nc.scalar.copy(staged[:], acc[:, 0:width])
-            nc.vector.tensor_copy(by_token[pool, t][:].indirect(offsets(pool, experts)), staged[:])
+            nc.vector.tensor_copy(by_token[pool, t][:].indirect(offsets(pool, slots)), staged[:])
 
         side_by_side = []
         for u, part in enumerate(PARTS):
@@ -157,20 +164,21 @@ def tile_moe_pool_relu_kernel(
         def product(engine, dst, t, tokens):
             engine.tensor_tensor(dst, by_token[POOL_A, t][:, tokens], by_token[POOL_C, t][:, tokens], MULT)
 
-        put_back(POOL_A, [0], 0)
-        put_back(POOL_A, both, 1)
-        put_back(POOL_A, [1], 0)
-        put_back(POOL_A, both, 2)
+        put_back(POOL_A, slice(0, FIRST_SLOTS), 0)
+        put_back(POOL_A, slice(0, SLOTS_PER_EXPERT), 1)
+        put_back(POOL_A, slice(FIRST_SLOTS, T), 0)
+        put_back(POOL_A, slice(SLOTS_PER_EXPERT, T), 1)
+        put_back(POOL_A, all_slots, 2)
         for t in range(LAST):
-            put_back(POOL_C, both, t)
+            put_back(POOL_C, all_slots, t)
             for u, part in enumerate(PARTS):
                 product(nc.gpsimd, side_by_side[u][:, :, t], t, part)
-        put_back(POOL_A, both, LAST)
+        put_back(POOL_A, all_slots, LAST)
 
-        open_window(POOL_C, LAST)
-        put_back(POOL_C, both, LAST)
+        open_window(POOL_C, LAST, f"window_c{LAST - 1}")
+        put_back(POOL_C, all_slots, LAST)
 
-        last_plane = held.tile([P, T], BF16, name="last_plane", align_bytes=64)
+        last_plane = held.tile([P, PARTS[PARTS_ON_SCALAR[-1]].stop], BF16, name="last_plane", align_bytes=64)
         for tokens in (PARTS[0], slice(PARTS[1].start, PARTS[2].stop)):
             product(nc.vector, last_plane[:, tokens], LAST, tokens)
         for u in PARTS_ON_SCALAR:
@@ -194,7 +202,7 @@ def tile_moe_pool_relu_kernel(
                 nc.tensor.matmul_mx(
                     out=total[:, PARTS[u].start - tokens.start : PARTS[u].stop - tokens.start],
                     lhsT=w2_codes[:].bitcast(FP8X4),
-                    lhsT_scale=w2_plane[:],
+                    lhsT_scale=w2_scale_tile[:],
                     rhs=h_words[:].bitcast(FP8X4),
                     rhs_scale=h_scales[:],
                     start=True,

@@ -23,11 +23,11 @@ QUADRANTS = 4
 POOL_A, POOL_C = 0, 1
 WINDOW = 704
 FIRST_SLOTS = 128
-PARTS = [slice(0, 128), slice(128, 256), slice(256, 320), slice(320, 448), slice(448, 512)]
+PARTS = [slice(0, 128), slice(320, 448), slice(448, 512), slice(128, 192), slice(192, 320)]
 PARTS_ON_SCALAR = [0, 1, 2]
 PARTS_ON_VECTOR = [3, 4]
-BANKS = [[0], [3, 4], [1], [2]]
-STORES = {0: [0], 4: [3, 4], 2: [1, 2]}
+PART_ORDER = [3, 0, 4, 1, 2]
+STORES = {0: slice(0, 192), 2: slice(192, 512)}
 
 
 def tile_moe_pool_relu_kernel(
@@ -178,7 +178,7 @@ def tile_moe_pool_relu_kernel(
         open_window(POOL_C, LAST, f"window_c{LAST - 1}")
         put_back(POOL_C, all_slots, LAST)
 
-        last_plane = held.tile([P, PARTS[PARTS_ON_SCALAR[-1]].stop], BF16, name="last_plane", align_bytes=64)
+        last_plane = held.tile([P, T], BF16, name="last_plane", align_bytes=64)
         for tokens in (PARTS[0], slice(PARTS[1].start, PARTS[2].stop)):
             product(nc.vector, last_plane[:, tokens], LAST, tokens)
         for u in PARTS_ON_SCALAR:
@@ -187,32 +187,28 @@ def tile_moe_pool_relu_kernel(
             product(nc.vector, side_by_side[u][:, :, LAST], LAST, PARTS[u])
 
         result = held.tile([N, T], F32, name="result")
-        for b, bank_parts in enumerate(BANKS):
-            tokens = slice(PARTS[bank_parts[0]].start, PARTS[bank_parts[-1]].stop)
-            total = ps_out.tile([N, tokens.stop - tokens.start], F32, name=f"total{b}")
-            for u in bank_parts:
-                width = PARTS[u].stop - PARTS[u].start
-                h_words = held.tile([P, width], U32, name=f"h_words{u}", align_bytes=64)
-                h_scales = held.tile([P, width], U8, name=f"h_scales{u}", align_bytes=64)
-                nc.vector.quantize_mx(
-                    out=h_words[:].bitcast(FP8X4),
-                    scales=h_scales[:],
-                    in_=side_by_side[u][:].rearrange("p c t -> p (c t)"),
-                )
-                nc.tensor.matmul_mx(
-                    out=total[:, PARTS[u].start - tokens.start : PARTS[u].stop - tokens.start],
-                    lhsT=w2_codes[:].bitcast(FP8X4),
-                    lhsT_scale=w2_scale_tile[:],
-                    rhs=h_words[:].bitcast(FP8X4),
-                    rhs_scale=h_scales[:],
-                    start=True,
-                    stop=True,
-                )
-            if b < len(BANKS) - 1:
-                nc.scalar.copy(result[:, tokens], total[:])
+        for u in PART_ORDER:
+            width = PARTS[u].stop - PARTS[u].start
+            total = ps_out.tile([N, width], F32, name=f"total{u}")
+            h_words = held.tile([P, width], U32, name=f"h_words{u}", align_bytes=64)
+            h_scales = held.tile([P, width], U8, name=f"h_scales{u}", align_bytes=64)
+            nc.vector.quantize_mx(
+                out=h_words[:].bitcast(FP8X4),
+                scales=h_scales[:],
+                in_=side_by_side[u][:].rearrange("p c t -> p (c t)"),
+            )
+            nc.tensor.matmul_mx(
+                out=total[:],
+                lhsT=w2_codes[:].bitcast(FP8X4),
+                lhsT_scale=w2_scale_tile[:],
+                rhs=h_words[:].bitcast(FP8X4),
+                rhs_scale=h_scales[:],
+                start=True,
+                stop=True,
+            )
+            if u == PART_ORDER[-1]:
+                nc.vector.tensor_copy(result[:, PARTS[u]], total[:])
             else:
-                nc.vector.tensor_copy(result[:, tokens], total[:])
-            if bank_parts[-1] in STORES:
-                stored = STORES[bank_parts[-1]]
-                columns = slice(PARTS[stored[0]].start, PARTS[stored[-1]].stop)
-                nc.sync.dma_start(out[:, columns], result[:, columns])
+                nc.scalar.copy(result[:, PARTS[u]], total[:])
+            if u in STORES:
+                nc.sync.dma_start(out[:, STORES[u]], result[:, STORES[u]])

@@ -23,11 +23,11 @@ QUADRANTS = 4
 POOL_A, POOL_C = 0, 1
 WINDOW = 704
 FIRST_SLOTS = 128
-PARTS = [slice(0, 128), slice(320, 448), slice(448, 512), slice(128, 192), slice(192, 320)]
+PARTS = [slice(0, 128), slice(320, 448), slice(448, 512), slice(256, 320), slice(128, 256)]
 PARTS_ON_SCALAR = [0, 1, 2]
-PARTS_ON_VECTOR = [3, 4]
-PART_ORDER = [3, 0, 4, 1, 2]
-STORES = {0: slice(0, 192), 2: slice(192, 512)}
+PARTS_ON_VECTOR = [4, 3]
+PART_ORDER = [4, 0, 3, 1, 2]
+STORES = {0: slice(0, 256), 2: slice(256, 512)}
 
 
 def tile_moe_pool_relu_kernel(

@@ -1,6 +1,7 @@
 from contextlib import ExitStack
 
 import concourse.mybir as mybir
+from concourse.masks import make_identity
 
 K, T, H, N = 512, 512, 512, 128
 EXPERTS, SLOTS_PER_EXPERT = 2, 256
@@ -23,11 +24,16 @@ QUADRANTS = 4
 POOL_A, POOL_C = 0, 1
 WINDOW = 704
 FIRST_SLOTS = 128
-PARTS = [slice(0, 128), slice(320, 448), slice(448, 512), slice(256, 320), slice(128, 256)]
-PARTS_ON_SCALAR = [0, 1, 2]
-PARTS_ON_VECTOR = [4, 3]
-PART_ORDER = [4, 0, 3, 1, 2]
-STORES = {0: slice(0, 256), 2: slice(256, 512)}
+VECTOR_STEPPED = [slice(128, 256)]
+VECTOR_PLAIN = [slice(256, 384), slice(384, 512)]
+GPSIMD_STEPPED = [slice(0, 128)]
+GPSIMD_PLAIN = []
+SCALAR_COPIES = [slice(256, 384), slice(384, 448), slice(448, 512)]
+TURNED = slice(128, 512)
+QUANTISED = [slice(0, 128), slice(128, 256), slice(256, 384), slice(384, 448), slice(448, 512)]
+PARTS = [slice(0, 128), slice(128, 256), slice(256, 384), slice(384, 448), slice(448, 512)]
+EMPTIED_BY_VECTOR = [4]
+STORES = {1: slice(0, 256), 4: slice(256, 512)}
 
 
 def tile_moe_pool_relu_kernel(
@@ -156,10 +162,9 @@ def tile_moe_pool_relu_kernel(
                 nc.scalar.copy(staged[:], acc[:, 0:width])
             nc.vector.tensor_copy(by_token[pool, t][:].indirect(offsets(pool, slots)), staged[:])
 
-        side_by_side = []
-        for u, part in enumerate(PARTS):
-            tile = held.tile([P, part.stop - part.start, PACK], BF16, name=f"side_by_side{u}", align_bytes=64)
-            side_by_side.append(tile)
+        side_by_side = held.tile([P, T, PACK], BF16, name="side_by_side", align_bytes=64)
+        identity = held.tile([P, P], F32, name="identity", align_bytes=64)
+        make_identity(nc, identity[:])
 
         def product(engine, dst, t, tokens):
             engine.tensor_tensor(dst, by_token[POOL_A, t][:, tokens], by_token[POOL_C, t][:, tokens], MULT)
@@ -171,44 +176,68 @@ def tile_moe_pool_relu_kernel(
         put_back(POOL_A, all_slots, 2)
         for t in range(LAST):
             put_back(POOL_C, all_slots, t)
-            for u, part in enumerate(PARTS):
-                product(nc.gpsimd, side_by_side[u][:, :, t], t, part)
+            product(nc.gpsimd, side_by_side[:, :, t], t, all_slots)
         put_back(POOL_A, all_slots, LAST)
 
         open_window(POOL_C, LAST, f"window_c{LAST - 1}")
         put_back(POOL_C, all_slots, LAST)
 
-        last_plane = held.tile([P, T], BF16, name="last_plane", align_bytes=64)
-        for tokens in (PARTS[0], slice(PARTS[1].start, PARTS[2].stop)):
-            product(nc.vector, last_plane[:, tokens], LAST, tokens)
-        for u in PARTS_ON_SCALAR:
-            nc.scalar.copy(side_by_side[u][:, :, LAST], last_plane[:, PARTS[u]])
-        for u in PARTS_ON_VECTOR:
-            product(nc.vector, side_by_side[u][:, :, LAST], LAST, PARTS[u])
+        n_turned = TURNED.stop - TURNED.start
+        once = ps_sums.tile([P, T], F32, name="once", tag=f"acc{len(put_back_so_far) % 2}")
+        rows = held.tile([P, T], F32, name="rows", tag="rows", align_bytes=64)
+        twice = ps_out.tile([P, n_turned], F32, name="twice")
+        for b in range(0, n_turned, P):
+            nc.tensor.transpose(
+                once[:, b : b + P], by_token[POOL_A, LAST][:, TURNED.start + b : TURNED.start + b + P], identity[:]
+            )
+        nc.scalar.copy(rows[:, 0:n_turned], once[:, 0:n_turned])
+        for b in range(0, n_turned, P):
+            nc.tensor.transpose(twice[:, b : b + P], rows[:, b : b + P], identity[:])
 
+        def product_from_psum(dst, tokens):
+            turned = twice[:, tokens.start - TURNED.start : tokens.stop - TURNED.start]
+            nc.vector.tensor_tensor(dst, by_token[POOL_C, LAST][:, tokens], turned, MULT)
+
+        last_plane = held.tile([P, T], BF16, name="last_plane", align_bytes=64)
+        for tokens in VECTOR_PLAIN:
+            product_from_psum(last_plane[:, tokens], tokens)
+        for tokens in GPSIMD_PLAIN:
+            product(nc.gpsimd, last_plane[:, tokens], LAST, tokens)
+        for tokens in GPSIMD_STEPPED:
+            product(nc.gpsimd, side_by_side[:, tokens, LAST], LAST, tokens)
+        for tokens in SCALAR_COPIES:
+            nc.scalar.copy(side_by_side[:, tokens, LAST], last_plane[:, tokens])
+        for tokens in VECTOR_STEPPED:
+            product_from_psum(side_by_side[:, tokens, LAST], tokens)
+
+        h_words = held.tile([P, T], U32, name="h_words", tag="rows", align_bytes=64)
+        h_scales = held.tile([P, T], U8, name="h_scales", align_bytes=64)
         result = held.tile([N, T], F32, name="result")
-        for u in PART_ORDER:
-            width = PARTS[u].stop - PARTS[u].start
-            total = ps_out.tile([N, width], F32, name=f"total{u}")
-            h_words = held.tile([P, width], U32, name=f"h_words{u}", align_bytes=64)
-            h_scales = held.tile([P, width], U8, name=f"h_scales{u}", align_bytes=64)
+        waiting = list(enumerate(PARTS))
+        done = set()
+        for tokens in QUANTISED:
             nc.vector.quantize_mx(
-                out=h_words[:].bitcast(FP8X4),
-                scales=h_scales[:],
-                in_=side_by_side[u][:].rearrange("p c t -> p (c t)"),
+                out=h_words[:, tokens].bitcast(FP8X4),
+                scales=h_scales[:, tokens],
+                in_=side_by_side[:, tokens, :].rearrange("p c t -> p (c t)"),
             )
-            nc.tensor.matmul_mx(
-                out=total[:],
-                lhsT=w2_codes[:].bitcast(FP8X4),
-                lhsT_scale=w2_scale_tile[:],
-                rhs=h_words[:].bitcast(FP8X4),
-                rhs_scale=h_scales[:],
-                start=True,
-                stop=True,
-            )
-            if u == PART_ORDER[-1]:
-                nc.vector.tensor_copy(result[:, PARTS[u]], total[:])
-            else:
-                nc.scalar.copy(result[:, PARTS[u]], total[:])
-            if u in STORES:
-                nc.sync.dma_start(out[:, STORES[u]], result[:, STORES[u]])
+            done = done | set(range(tokens.start, tokens.stop))
+            for u, part in list(waiting):
+                if set(range(part.start, part.stop)) <= done:
+                    waiting.remove((u, part))
+                    total = ps_out.tile([N, part.stop - part.start], F32, name=f"total{u}")
+                    nc.tensor.matmul_mx(
+                        out=total[:],
+                        lhsT=w2_codes[:].bitcast(FP8X4),
+                        lhsT_scale=w2_scale_tile[:],
+                        rhs=h_words[:, part].bitcast(FP8X4),
+                        rhs_scale=h_scales[:, part],
+                        start=True,
+                        stop=True,
+                    )
+                    if u in EMPTIED_BY_VECTOR:
+                        nc.vector.tensor_copy(result[:, part], total[:])
+                    else:
+                        nc.scalar.copy(result[:, part], total[:])
+                    if u in STORES:
+                        nc.sync.dma_start(out[:, STORES[u]], result[:, STORES[u]])

@@ -25,15 +25,15 @@ POOL_A, POOL_C = 0, 1
 WINDOW = 704
 FIRST_SLOTS = 128
 VECTOR_STEPPED = [slice(128, 256)]
-VECTOR_PLAIN = [slice(256, 384), slice(384, 512)]
+VECTOR_PLAIN = [slice(256, 320), slice(320, 512)]
 GPSIMD_STEPPED = [slice(0, 128)]
 GPSIMD_PLAIN = []
-SCALAR_COPIES = [slice(256, 384), slice(384, 448), slice(448, 512)]
+SCALAR_COPIES = [slice(256, 320), slice(320, 448), slice(448, 512)]
 TURNED = slice(128, 512)
-QUANTISED = [slice(0, 128), slice(128, 256), slice(256, 384), slice(384, 448), slice(448, 512)]
-PARTS = [slice(0, 128), slice(128, 256), slice(256, 384), slice(384, 448), slice(448, 512)]
+QUANTISED = [slice(0, 128), slice(128, 256), slice(256, 320), slice(320, 448), slice(448, 512)]
+PARTS = [slice(0, 128), slice(128, 256), slice(256, 320), slice(320, 448), slice(448, 512)]
 EMPTIED_BY_VECTOR = [4]
-STORES = {1: slice(0, 256), 4: slice(256, 512)}
+STORES = {2: slice(0, 320), 4: slice(320, 512)}
 
 
 def tile_moe_pool_relu_kernel(

@@ -1,10 +1,9 @@
 from contextlib import ExitStack
 
 import concourse.mybir as mybir
-from concourse.masks import make_identity
 
 K, T, H, N = 512, 512, 512, 128
-EXPERTS, SLOTS_PER_EXPERT = 2, 256
+EXPERTS, SLOTS = 2, 256
 FLOPS = 2 * (2 * K * H * T) + 2 * H * N * T
 
 F32 = mybir.dt.float32
@@ -15,6 +14,7 @@ U16 = mybir.dt.uint16
 U8 = mybir.dt.uint8
 FP8X4 = mybir.dt.float8_e4m3fn_x4
 RELU = mybir.ActivationFunctionType.Relu
+COPY = mybir.ActivationFunctionType.Copy
 MULT = mybir.AluOpType.mult
 
 P = 128
@@ -23,17 +23,12 @@ LAST = PACK - 1
 QUADRANTS = 4
 POOL_A, POOL_C = 0, 1
 WINDOW = 704
-FIRST_SLOTS = 128
-VECTOR_STEPPED = [slice(128, 256)]
-VECTOR_PLAIN = [slice(256, 320), slice(320, 512)]
-GPSIMD_STEPPED = [slice(0, 128)]
-GPSIMD_PLAIN = []
-SCALAR_COPIES = [slice(256, 320), slice(320, 448), slice(448, 512)]
-TURNED = slice(128, 512)
-QUANTISED = [slice(0, 128), slice(128, 256), slice(256, 320), slice(320, 448), slice(448, 512)]
-PARTS = [slice(0, 128), slice(128, 256), slice(256, 320), slice(320, 448), slice(448, 512)]
-EMPTIED_BY_VECTOR = [4]
-STORES = {2: slice(0, 320), 4: slice(320, 512)}
+PRODUCTS = [slice(256, 512), slice(0, 256)]
+SCALAR_COPIES = [slice(256, 384), slice(384, 512)]
+VECTOR_COPIES = [slice(0, 128), slice(128, 256)]
+PARTS = [slice(0, 128), slice(128, 256), slice(256, 384), slice(384, 512)]
+EMPTIED_BY_VECTOR = [3]
+STORES = {1: slice(0, 256), 3: slice(256, 512)}
 
 
 def tile_moe_pool_relu_kernel(
@@ -42,8 +37,7 @@ def tile_moe_pool_relu_kernel(
     nc = tc.nc
     with ExitStack() as ctx:
         held = ctx.enter_context(tc.tile_pool(name="held", bufs=1))
-        ps_sums = ctx.enter_context(tc.psum_pool(name="ps_sums", bufs=1))
-        ps_out = ctx.enter_context(tc.psum_pool(name="ps_out", bufs=1))
+        banks = ctx.enter_context(tc.psum_pool(name="banks", bufs=1))
 
         def as_words(dram):
             return dram.rearrange("p c d -> p (c d)").bitcast(I32)
@@ -77,167 +71,153 @@ def tile_moe_pool_relu_kernel(
         nc.sync.dma_start(lists[POOL_A][:], offs)
         token_scales = load_scales_repeated("token_scales", x_scales[0], [nc.scalar, nc.sync, nc.scalar, nc.sync], WINDOW)
         token_words = load_words("token_words", x_words[0], nc.scalar, WINDOW)
-        wa_codes = held.tile([P, EXPERTS, H], I32, name="wa_codes", align_bytes=64)
-        nc.scalar.dma_start(wa_codes[:, 0, :], as_words(wa_words[0, 0]))
+        codes = {}
+        codes[POOL_A, 0] = load_words("wa0_codes", wa_words[0, 0], nc.scalar, H)
         nc.sync.dma_start(lists[POOL_C][:], offs2)
         load_pool_scales(POOL_A, wa_scales)
-        nc.sync.dma_start(wa_codes[:, 1, :], as_words(wa_words[1, 0]))
-        wb0_codes = load_words("wb0_codes", wb_words[0, 0], nc.sync, H)
+        codes[POOL_C, 0] = load_words("wb0_codes", wb_words[0, 0], nc.sync, H)
+        codes[POOL_C, 1] = load_words("wb1_codes", wb_words[1, 0], nc.sync, H)
         load_pool_scales(POOL_C, wb_scales)
-        wb1_codes = load_words("wb1_codes", wb_words[1, 0], nc.sync, H)
+        codes[POOL_A, 1] = load_words("wa1_codes", wa_words[1, 0], nc.sync, H)
         w2_codes = load_words("w2_codes", w2_words[0], nc.sync, N)
         w2_scale_tile = load_scales_repeated("w2_scale_tile", w2_scales[0], [nc.sync] * QUADRANTS, N)
 
-        def sort_columns(into, name, source, dtype, planes):
+        def sort_columns(copy, into, name, source, dtype, planes):
             tile = held.tile([P, len(planes), P], dtype, name=f"{name}_{planes[0]}", align_bytes=64)
             by_plane = source.bitcast(dtype).rearrange("k (p t) -> k t p", t=PACK)
-            nc.gpsimd.tensor_copy(tile[:], by_plane[:, planes[0] : planes[-1] + 1, :])
+            copy(tile[:], by_plane[:, planes[0] : planes[-1] + 1, :])
             for n, t in enumerate(planes):
                 into[t] = tile[:, n, :]
 
         sorted_words = {(pool, e): {} for pool in (POOL_A, POOL_C) for e in range(EXPERTS)}
         sorted_scales = {POOL_A: {}, POOL_C: {}}
-
         early, late = [0, 1], [2, 3]
-        for t in early:
-            sort_columns(sorted_words[POOL_A, 0], "sorted_wa0", wa_codes[:, 0, :], U32, [t])
-        for t in early:
-            sort_columns(sorted_scales[POOL_A], "sorted_sa", pool_scales[POOL_A][:], U8, [t])
-        for t in early:
-            sort_columns(sorted_words[POOL_A, 1], "sorted_wa1", wa_codes[:, 1, :], U32, [t])
-        sort_columns(sorted_scales[POOL_A], "sorted_sa", pool_scales[POOL_A][:], U8, late)
-        wa_late = held.tile([P, EXPERTS, len(late), P], U32, name="wa_late", align_bytes=64)
-        wa_by_plane = wa_codes[:].bitcast(U32).rearrange("k e (p t) -> k e t p", t=PACK)
-        nc.gpsimd.tensor_copy(wa_late[:], wa_by_plane[:, :, late[0] : PACK, :])
+        sort_columns(nc.scalar.copy, sorted_words[POOL_A, 0], "sorted_wa0", codes[POOL_A, 0][:], U32, early + late)
+        for planes in (early, late):
+            sort_columns(nc.gpsimd.tensor_copy, sorted_scales[POOL_A], "sorted_sa", pool_scales[POOL_A][:], U8, planes)
         for e in range(EXPERTS):
-            for n, t in enumerate(late):
-                sorted_words[POOL_A, e][t] = wa_late[:, e, n, :]
-        sort_columns(sorted_words[POOL_C, 0], "sorted_wb0", wb0_codes[:], U32, early + late)
-        sort_columns(sorted_words[POOL_C, 1], "sorted_wb1", wb1_codes[:], U32, early + late)
-        sort_columns(sorted_scales[POOL_C], "sorted_sb", pool_scales[POOL_C][:], U8, early + late)
+            sort_columns(nc.gpsimd.tensor_copy, sorted_words[POOL_C, e], f"sorted_wb{e}", codes[POOL_C, e][:], U32, early)
+        sort_columns(nc.gpsimd.tensor_copy, sorted_scales[POOL_C], "sorted_sb", pool_scales[POOL_C][:], U8, early)
+        sort_columns(nc.gpsimd.tensor_copy, sorted_words[POOL_A, 1], "sorted_wa1", codes[POOL_A, 1][:], U32, early + late)
+        for e in range(EXPERTS):
+            sort_columns(nc.gpsimd.tensor_copy, sorted_words[POOL_C, e], f"sorted_wb{e}", codes[POOL_C, e][:], U32, late)
+        sort_columns(nc.gpsimd.tensor_copy, sorted_scales[POOL_C], "sorted_sb", pool_scales[POOL_C][:], U8, late)
 
         def offsets(pool, slots):
             return lists[pool][:, slots.start // 16 : slots.stop // 16]
 
-        all_slots = slice(0, T)
+        def expert_slots(e):
+            return slice(e * SLOTS, (e + 1) * SLOTS)
+
         slot_words, slot_scales = {}, {}
         for pool in (POOL_A, POOL_C):
             slot_scales[pool] = held.tile([P, T], U8, name=f"slot_scales{pool}", align_bytes=64)
             slot_words[pool] = held.tile([P, T], U32, name=f"slot_words{pool}", align_bytes=64)
-            nc.vector.tensor_copy(slot_scales[pool][:], token_scales[:].indirect(offsets(pool, all_slots)))
-            nc.vector.tensor_copy(slot_words[pool][:], token_words[:].bitcast(U32).indirect(offsets(pool, all_slots)))
+
+        def gather(pool, slots):
+            nc.vector.tensor_copy(slot_scales[pool][:, slots], token_scales[:].indirect(offsets(pool, slots)))
+            nc.vector.tensor_copy(slot_words[pool][:, slots], token_words[:].bitcast(U32).indirect(offsets(pool, slots)))
+
+        all_slots = slice(0, T)
+        gather(POOL_A, expert_slots(0))
+        gather(POOL_C, all_slots)
+        gather(POOL_A, expert_slots(1))
 
         by_token = {}
-
-        def open_window(pool, t, tag):
-            by_token[pool, t] = held.tile([P, WINDOW], F32, name=f"by_token{pool}{t}", tag=tag, align_bytes=64)
-
         for t in range(PACK):
-            open_window(POOL_A, t, f"window_a{t}")
-        for t in range(LAST):
-            open_window(POOL_C, t, f"window_c{t}")
+            by_token[POOL_A, t] = held.tile([P, T], F32, name=f"a_by_token{t}", align_bytes=64)
+            by_token[POOL_C, t] = held.tile([P, WINDOW], F32, name=f"c_by_token{t}", tag=f"window_c{t}", align_bytes=64)
 
-        put_back_so_far = []
+        def sums(pool, pieces, tag):
+            acc = banks.tile([P, T], F32, name="acc", tag=tag)
+            for n, (t, e) in enumerate(pieces):
+                nc.tensor.matmul_mx(
+                    out=acc[:, n * SLOTS : (n + 1) * SLOTS],
+                    lhsT=sorted_words[pool, e][t].bitcast(FP8X4),
+                    lhsT_scale=sorted_scales[pool][t][4 * e :, :],
+                    rhs=slot_words[pool][:, expert_slots(e)].bitcast(FP8X4),
+                    rhs_scale=slot_scales[pool][:, expert_slots(e)],
+                    start=True,
+                    stop=True,
+                )
+            return acc
 
-        def put_back(pool, slots, t):
-            width = slots.stop - slots.start
-            acc = ps_sums.tile([P, T], F32, name="acc", tag=f"acc{len(put_back_so_far) % 2}")
-            put_back_so_far.append((pool, slots, t))
-            for e in range(EXPERTS):
-                first, stop = max(slots.start, e * SLOTS_PER_EXPERT), min(slots.stop, (e + 1) * SLOTS_PER_EXPERT)
-                if first < stop:
-                    nc.tensor.matmul_mx(
-                        out=acc[:, first - slots.start : stop - slots.start],
-                        lhsT=sorted_words[pool, e][t].bitcast(FP8X4),
-                        lhsT_scale=sorted_scales[pool][t][4 * e :, :],
-                        rhs=slot_words[pool][:, first:stop].bitcast(FP8X4),
-                        rhs_scale=slot_scales[pool][:, first:stop],
-                        start=True,
-                        stop=True,
-                    )
-            staged = held.tile([P, width], F32, name=f"staged{pool}_{slots.start}_{t}", align_bytes=64)
-            if pool == POOL_A:
-                nc.scalar.activation(staged[:], acc[:, 0:width], RELU)
-            else:
-                nc.scalar.copy(staged[:], acc[:, 0:width])
-            nc.vector.tensor_copy(by_token[pool, t][:].indirect(offsets(pool, slots)), staged[:])
+        staged_a, staged_c = {}, {}
+
+        def stage_a(planes, e, tag):
+            acc = sums(POOL_A, [(t, e) for t in planes], tag)
+            staged = held.tile([P, T], F32, name=f"staged_a{planes[0]}{e}", align_bytes=64)
+            nc.scalar.activation(staged[:], acc[:], RELU)
+            for n, t in enumerate(planes):
+                staged_a[t, e] = staged[:, n * SLOTS : (n + 1) * SLOTS]
+
+        def stage_c(t, copy, tag):
+            acc = sums(POOL_C, [(t, e) for e in range(EXPERTS)], tag)
+            staged_c[t] = held.tile([P, T], F32, name=f"staged_c{t}", align_bytes=64)
+            copy(staged_c[t][:], acc[:])
+
+        def scatter_a(t, e):
+            nc.scalar.activation(by_token[POOL_A, t][:].indirect(offsets(POOL_A, expert_slots(e))), staged_a[t, e], COPY)
+
+        def scatter_c(t):
+            nc.vector.tensor_copy(by_token[POOL_C, t][:].indirect(offsets(POOL_C, all_slots)), staged_c[t][:])
 
         side_by_side = held.tile([P, T, PACK], BF16, name="side_by_side", align_bytes=64)
-        identity = held.tile([P, P], F32, name="identity", align_bytes=64)
-        make_identity(nc, identity[:])
 
         def product(engine, dst, t, tokens):
             engine.tensor_tensor(dst, by_token[POOL_A, t][:, tokens], by_token[POOL_C, t][:, tokens], MULT)
 
-        put_back(POOL_A, slice(0, FIRST_SLOTS), 0)
-        put_back(POOL_A, slice(0, SLOTS_PER_EXPERT), 1)
-        put_back(POOL_A, slice(FIRST_SLOTS, T), 0)
-        put_back(POOL_A, slice(SLOTS_PER_EXPERT, T), 1)
-        put_back(POOL_A, all_slots, 2)
-        for t in range(LAST):
-            put_back(POOL_C, all_slots, t)
-            product(nc.gpsimd, side_by_side[:, :, t], t, all_slots)
-        put_back(POOL_A, all_slots, LAST)
+        stage_a(early, 0, "bank0")
+        stage_a(late, 0, "bank1")
+        for t in early:
+            stage_c(t, nc.vector.tensor_copy, f"bank{2 + t}")
+        for t in early:
+            scatter_a(t, 0)
+        stage_a(early, 1, "bank4")
+        stage_a(late, 1, "bank5")
+        for t in late:
+            stage_c(t, nc.scalar.copy, f"bank{2 + t}")
+        for t in early:
+            scatter_a(t, 1)
+        for t in late:
+            scatter_a(t, 0)
+        for t in late:
+            scatter_a(t, 1)
+        for t in range(PACK):
+            scatter_c(t)
+            if t < LAST:
+                product(nc.gpsimd, side_by_side[:, :, t], t, all_slots)
 
-        open_window(POOL_C, LAST, f"window_c{LAST - 1}")
-        put_back(POOL_C, all_slots, LAST)
-
-        n_turned = TURNED.stop - TURNED.start
-        once = ps_sums.tile([P, T], F32, name="once", tag=f"acc{len(put_back_so_far) % 2}")
-        rows = held.tile([P, T], F32, name="rows", tag="rows", align_bytes=64)
-        twice = ps_out.tile([P, n_turned], F32, name="twice")
-        for b in range(0, n_turned, P):
-            nc.tensor.transpose(
-                once[:, b : b + P], by_token[POOL_A, LAST][:, TURNED.start + b : TURNED.start + b + P], identity[:]
-            )
-        nc.scalar.copy(rows[:, 0:n_turned], once[:, 0:n_turned])
-        for b in range(0, n_turned, P):
-            nc.tensor.transpose(twice[:, b : b + P], rows[:, b : b + P], identity[:])
-
-        def product_from_psum(dst, tokens):
-            turned = twice[:, tokens.start - TURNED.start : tokens.stop - TURNED.start]
-            nc.vector.tensor_tensor(dst, by_token[POOL_C, LAST][:, tokens], turned, MULT)
-
-        last_plane = held.tile([P, T], BF16, name="last_plane", align_bytes=64)
-        for tokens in VECTOR_PLAIN:
-            product_from_psum(last_plane[:, tokens], tokens)
-        for tokens in GPSIMD_PLAIN:
-            product(nc.gpsimd, last_plane[:, tokens], LAST, tokens)
-        for tokens in GPSIMD_STEPPED:
-            product(nc.gpsimd, side_by_side[:, tokens, LAST], LAST, tokens)
+        last_plane = held.tile([P, T], BF16, name="last_plane", tag=f"window_c{LAST - 1}", align_bytes=64)
+        for tokens in PRODUCTS:
+            product(nc.vector, last_plane[:, tokens], LAST, tokens)
         for tokens in SCALAR_COPIES:
             nc.scalar.copy(side_by_side[:, tokens, LAST], last_plane[:, tokens])
-        for tokens in VECTOR_STEPPED:
-            product_from_psum(side_by_side[:, tokens, LAST], tokens)
+        for tokens in VECTOR_COPIES:
+            nc.vector.tensor_copy(side_by_side[:, tokens, LAST], last_plane[:, tokens])
 
-        h_words = held.tile([P, T], U32, name="h_words", tag="rows", align_bytes=64)
+        h_words = held.tile([P, T], U32, name="h_words", align_bytes=64)
         h_scales = held.tile([P, T], U8, name="h_scales", align_bytes=64)
         result = held.tile([N, T], F32, name="result")
-        waiting = list(enumerate(PARTS))
-        done = set()
-        for tokens in QUANTISED:
+        for u, tokens in enumerate(PARTS):
             nc.vector.quantize_mx(
                 out=h_words[:, tokens].bitcast(FP8X4),
                 scales=h_scales[:, tokens],
                 in_=side_by_side[:, tokens, :].rearrange("p c t -> p (c t)"),
             )
-            done = done | set(range(tokens.start, tokens.stop))
-            for u, part in list(waiting):
-                if set(range(part.start, part.stop)) <= done:
-                    waiting.remove((u, part))
-                    total = ps_out.tile([N, part.stop - part.start], F32, name=f"total{u}")
-                    nc.tensor.matmul_mx(
-                        out=total[:],
-                        lhsT=w2_codes[:].bitcast(FP8X4),
-                        lhsT_scale=w2_scale_tile[:],
-                        rhs=h_words[:, part].bitcast(FP8X4),
-                        rhs_scale=h_scales[:, part],
-                        start=True,
-                        stop=True,
-                    )
-                    if u in EMPTIED_BY_VECTOR:
-                        nc.vector.tensor_copy(result[:, part], total[:])
-                    else:
-                        nc.scalar.copy(result[:, part], total[:])
-                    if u in STORES:
-                        nc.sync.dma_start(out[:, STORES[u]], result[:, STORES[u]])
+            total = banks.tile([N, tokens.stop - tokens.start], F32, name="total", tag=f"bank{u}")
+            nc.tensor.matmul_mx(
+                out=total[:],
+                lhsT=w2_codes[:].bitcast(FP8X4),
+                lhsT_scale=w2_scale_tile[:],
+                rhs=h_words[:, tokens].bitcast(FP8X4),
+                rhs_scale=h_scales[:, tokens],
+                start=True,
+                stop=True,
+            )
+            if u in EMPTIED_BY_VECTOR:
+                nc.vector.tensor_copy(result[:, tokens], total[:])
+            else:
+                nc.scalar.copy(result[:, tokens], total[:])
+            if u in STORES:
+                nc.sync.dma_start(out[:, STORES[u]], result[:, STORES[u]])

@@ -23,6 +23,8 @@ LAST = PACK - 1
 QUADRANTS = 4
 POOL_A, POOL_C = 0, 1
 WINDOW = 704
+LAST_CUT = 128
+SCALAR_SHARE = 160
 PRODUCTS = [slice(256, 512), slice(0, 256)]
 SCALAR_COPIES = [slice(256, 384), slice(384, 512)]
 VECTOR_COPIES = [slice(0, 128), slice(128, 256)]
@@ -61,23 +63,23 @@ def tile_moe_pool_relu_kernel(
             nc.gpsimd.memset(tile[:], 0)
             pool_scales.append(tile)
 
-        def load_pool_scales(pool, dram):
-            for q in range(QUADRANTS):
-                nc.sync.dma_start(
+        def load_pool_scales(pool, dram, queues):
+            for q, queue in enumerate(queues):
+                queue.dma_start(
                     pool_scales[pool][32 * q : 32 * q + 4 * EXPERTS, :], dram[:, 0, 4 * q : 4 * q + 4, :].bitcast(I32)
                 )
 
         lists = [held.tile([P, T // 16], U16, name="list_a"), held.tile([P, T // 16], U16, name="list_c")]
         nc.sync.dma_start(lists[POOL_A][:], offs)
         token_scales = load_scales_repeated("token_scales", x_scales[0], [nc.scalar, nc.sync, nc.scalar, nc.sync], WINDOW)
+        nc.sync.dma_start(lists[POOL_C][:], offs2)
         token_words = load_words("token_words", x_words[0], nc.scalar, WINDOW)
         codes = {}
         codes[POOL_A, 0] = load_words("wa0_codes", wa_words[0, 0], nc.scalar, H)
-        nc.sync.dma_start(lists[POOL_C][:], offs2)
-        load_pool_scales(POOL_A, wa_scales)
-        codes[POOL_C, 0] = load_words("wb0_codes", wb_words[0, 0], nc.sync, H)
-        codes[POOL_C, 1] = load_words("wb1_codes", wb_words[1, 0], nc.sync, H)
-        load_pool_scales(POOL_C, wb_scales)
+        load_pool_scales(POOL_A, wa_scales, [nc.sync] * QUADRANTS)
+        load_pool_scales(POOL_C, wb_scales, [nc.sync, nc.sync, nc.gpsimd, nc.gpsimd])
+        wb_codes = held.tile([P, EXPERTS, H], I32, name="wb_codes", align_bytes=64)
+        nc.sync.dma_start(wb_codes[:], wb_words[:, 0].rearrange("e p c d -> p e (c d)").bitcast(I32))
         codes[POOL_A, 1] = load_words("wa1_codes", wa_words[1, 0], nc.sync, H)
         w2_codes = load_words("w2_codes", w2_words[0], nc.sync, N)
         w2_scale_tile = load_scales_repeated("w2_scale_tile", w2_scales[0], [nc.sync] * QUADRANTS, N)
@@ -93,15 +95,22 @@ def tile_moe_pool_relu_kernel(
         sorted_scales = {POOL_A: {}, POOL_C: {}}
         early, late = [0, 1], [2, 3]
         sort_columns(nc.scalar.copy, sorted_words[POOL_A, 0], "sorted_wa0", codes[POOL_A, 0][:], U32, early + late)
-        for planes in (early, late):
+        for planes in ([0], [1, 2], [3]):
             sort_columns(nc.gpsimd.tensor_copy, sorted_scales[POOL_A], "sorted_sa", pool_scales[POOL_A][:], U8, planes)
-        for e in range(EXPERTS):
-            sort_columns(nc.gpsimd.tensor_copy, sorted_words[POOL_C, e], f"sorted_wb{e}", codes[POOL_C, e][:], U32, early)
-        sort_columns(nc.gpsimd.tensor_copy, sorted_scales[POOL_C], "sorted_sb", pool_scales[POOL_C][:], U8, early)
-        sort_columns(nc.gpsimd.tensor_copy, sorted_words[POOL_A, 1], "sorted_wa1", codes[POOL_A, 1][:], U32, early + late)
-        for e in range(EXPERTS):
-            sort_columns(nc.gpsimd.tensor_copy, sorted_words[POOL_C, e], f"sorted_wb{e}", codes[POOL_C, e][:], U32, late)
-        sort_columns(nc.gpsimd.tensor_copy, sorted_scales[POOL_C], "sorted_sb", pool_scales[POOL_C][:], U8, late)
+
+        def sort_wb(planes):
+            tile = held.tile([P, EXPERTS, len(planes), P], U32, name=f"sorted_wb_{planes[0]}", align_bytes=64)
+            by_plane = wb_codes[:].bitcast(U32).rearrange("k e (p t) -> k e t p", t=PACK)
+            nc.gpsimd.tensor_copy(tile[:], by_plane[:, :, planes[0] : planes[-1] + 1, :])
+            for e in range(EXPERTS):
+                for n, t in enumerate(planes):
+                    sorted_words[POOL_C, e][t] = tile[:, e, n, :]
+            sort_columns(nc.gpsimd.tensor_copy, sorted_scales[POOL_C], "sorted_sb", pool_scales[POOL_C][:], U8, planes)
+
+        sort_wb(early)
+        sort_wb(late)
+        for planes in (early, late):
+            sort_columns(nc.gpsimd.tensor_copy, sorted_words[POOL_A, 1], "sorted_wa1", codes[POOL_A, 1][:], U32, planes)
 
         def offsets(pool, slots):
             return lists[pool][:, slots.start // 16 : slots.stop // 16]
@@ -126,7 +135,12 @@ def tile_moe_pool_relu_kernel(
         by_token = {}
         for t in range(PACK):
             by_token[POOL_A, t] = held.tile([P, T], F32, name=f"a_by_token{t}", align_bytes=64)
-            by_token[POOL_C, t] = held.tile([P, WINDOW], F32, name=f"c_by_token{t}", tag=f"window_c{t}", align_bytes=64)
+
+        def open_window(t, tag):
+            by_token[POOL_C, t] = held.tile([P, WINDOW], F32, name=f"c_by_token{t}", tag=tag, align_bytes=64)
+
+        for t in range(LAST):
+            open_window(t, f"window_c{t}")
 
         def sums(pool, pieces, tag):
             acc = banks.tile([P, T], F32, name="acc", tag=tag)
@@ -142,51 +156,56 @@ def tile_moe_pool_relu_kernel(
                 )
             return acc
 
-        staged_a, staged_c = {}, {}
+        staged_a = held.tile([P, PACK, T], F32, name="staged_a", align_bytes=64)
+        staged_c = {}
 
         def stage_a(planes, e, tag):
             acc = sums(POOL_A, [(t, e) for t in planes], tag)
-            staged = held.tile([P, T], F32, name=f"staged_a{planes[0]}{e}", align_bytes=64)
-            nc.scalar.activation(staged[:], acc[:], RELU)
-            for n, t in enumerate(planes):
-                staged_a[t, e] = staged[:, n * SLOTS : (n + 1) * SLOTS]
+            filled = acc[:, 0 : len(planes) * SLOTS].rearrange("p (t s) -> p t s", s=SLOTS)
+            nc.scalar.activation(staged_a[:, planes[0] : planes[-1] + 1, expert_slots(e)], filled, RELU)
 
         def stage_c(t, copy, tag):
             acc = sums(POOL_C, [(t, e) for e in range(EXPERTS)], tag)
             staged_c[t] = held.tile([P, T], F32, name=f"staged_c{t}", align_bytes=64)
             copy(staged_c[t][:], acc[:])
 
-        def scatter_a(t, e):
-            nc.scalar.activation(by_token[POOL_A, t][:].indirect(offsets(POOL_A, expert_slots(e))), staged_a[t, e], COPY)
+        def scalar_scatter(window, source):
+            nc.scalar.activation(window, source, COPY)
 
-        def scatter_c(t):
-            nc.vector.tensor_copy(by_token[POOL_C, t][:].indirect(offsets(POOL_C, all_slots)), staged_c[t][:])
+        def scatter_a(t, slots, copy):
+            copy(by_token[POOL_A, t][:].indirect(offsets(POOL_A, slots)), staged_a[:, t, slots])
+
+        def scatter_c(t, slots, copy):
+            copy(by_token[POOL_C, t][:].indirect(offsets(POOL_C, slots)), staged_c[t][:, slots])
 
         side_by_side = held.tile([P, T, PACK], BF16, name="side_by_side", align_bytes=64)
 
         def product(engine, dst, t, tokens):
             engine.tensor_tensor(dst, by_token[POOL_A, t][:, tokens], by_token[POOL_C, t][:, tokens], MULT)
 
-        stage_a(early, 0, "bank0")
-        stage_a(late, 0, "bank1")
+        stage_a([0], 0, "bank0")
+        stage_a([1, 2], 0, "bank1")
+        scatter_a(2, expert_slots(0), nc.vector.tensor_copy)
         for t in early:
             stage_c(t, nc.vector.tensor_copy, f"bank{2 + t}")
         for t in early:
-            scatter_a(t, 0)
+            scatter_a(t, expert_slots(0), scalar_scatter)
+        stage_c(2, nc.scalar.copy, "bank5")
+        stage_c(3, nc.scalar.copy, "bank6")
+        scatter_c(2, slice(0, SCALAR_SHARE), scalar_scatter)
         stage_a(early, 1, "bank4")
-        stage_a(late, 1, "bank5")
-        for t in late:
-            stage_c(t, nc.scalar.copy, f"bank{2 + t}")
         for t in early:
-            scatter_a(t, 1)
-        for t in late:
-            scatter_a(t, 0)
-        for t in late:
-            scatter_a(t, 1)
-        for t in range(PACK):
-            scatter_c(t)
-            if t < LAST:
-                product(nc.gpsimd, side_by_side[:, :, t], t, all_slots)
+            scatter_a(t, expert_slots(1), scalar_scatter)
+        stage_a([3], 0, "bank4")
+        stage_a(late, 1, "bank5")
+        scatter_a(3, slice(0, LAST_CUT), scalar_scatter)
+        scatter_a(2, expert_slots(1), scalar_scatter)
+        scatter_a(3, slice(LAST_CUT, T), scalar_scatter)
+        for t in range(LAST):
+            scatter_c(t, slice(SCALAR_SHARE, T) if t == 2 else all_slots, nc.vector.tensor_copy)
+            product(nc.gpsimd, side_by_side[:, :, t], t, all_slots)
+        open_window(LAST, "window_c0")
+        scatter_c(LAST, all_slots, nc.vector.tensor_copy)
 
         last_plane = held.tile([P, T], BF16, name="last_plane", tag=f"window_c{LAST - 1}", align_bytes=64)
         for tokens in PRODUCTS:

@@ -25,12 +25,12 @@ POOL_A, POOL_C = 0, 1
 WINDOW = 704
 LAST_CUT = 128
 SCALAR_SHARE = 160
-PRODUCTS = [slice(256, 512), slice(0, 256)]
+PRODUCTS = [slice(256, 384), slice(0, 256), slice(384, 512)]
 SCALAR_COPIES = [slice(256, 384), slice(384, 512)]
-VECTOR_COPIES = [slice(0, 128), slice(128, 256)]
-PARTS = [slice(0, 128), slice(128, 256), slice(256, 384), slice(384, 512)]
+VECTOR_COPIES = [slice(0, 256)]
+PARTS = [slice(256, 384), slice(384, 512), slice(0, 128), slice(128, 256)]
 EMPTIED_BY_VECTOR = [3]
-STORES = {1: slice(0, 256), 3: slice(256, 512)}
+STORES = {1: slice(256, 512), 3: slice(0, 256)}
 
 
 def tile_moe_pool_relu_kernel(
@@ -98,19 +98,23 @@ def tile_moe_pool_relu_kernel(
         for planes in ([0], [1, 2], [3]):
             sort_columns(nc.gpsimd.tensor_copy, sorted_scales[POOL_A], "sorted_sa", pool_scales[POOL_A][:], U8, planes)
 
-        def sort_wb(planes):
+        def sort_wb_words(planes):
             tile = held.tile([P, EXPERTS, len(planes), P], U32, name=f"sorted_wb_{planes[0]}", align_bytes=64)
             by_plane = wb_codes[:].bitcast(U32).rearrange("k e (p t) -> k e t p", t=PACK)
             nc.gpsimd.tensor_copy(tile[:], by_plane[:, :, planes[0] : planes[-1] + 1, :])
             for e in range(EXPERTS):
                 for n, t in enumerate(planes):
                     sorted_words[POOL_C, e][t] = tile[:, e, n, :]
+
+        def sort_wb_scales(planes):
             sort_columns(nc.gpsimd.tensor_copy, sorted_scales[POOL_C], "sorted_sb", pool_scales[POOL_C][:], U8, planes)
 
-        sort_wb(early)
-        sort_wb(late)
-        for planes in (early, late):
-            sort_columns(nc.gpsimd.tensor_copy, sorted_words[POOL_A, 1], "sorted_wa1", codes[POOL_A, 1][:], U32, planes)
+        sort_wb_words(early)
+        sort_wb_scales(early)
+        sort_wb_words(late)
+        sort_columns(nc.gpsimd.tensor_copy, sorted_words[POOL_A, 1], "sorted_wa1", codes[POOL_A, 1][:], U32, early)
+        sort_wb_scales(late)
+        sort_columns(nc.gpsimd.tensor_copy, sorted_words[POOL_A, 1], "sorted_wa1", codes[POOL_A, 1][:], U32, late)
 
         def offsets(pool, slots):
             return lists[pool][:, slots.start // 16 : slots.stop // 16]
@@ -185,20 +189,20 @@ def tile_moe_pool_relu_kernel(
 
         stage_a([0], 0, "bank0")
         stage_a([1, 2], 0, "bank1")
+        stage_a([3], 0, "bank7")
         scatter_a(2, expert_slots(0), nc.vector.tensor_copy)
         for t in early:
             stage_c(t, nc.vector.tensor_copy, f"bank{2 + t}")
         for t in early:
             scatter_a(t, expert_slots(0), scalar_scatter)
+        scatter_a(3, slice(0, LAST_CUT), scalar_scatter)
+        stage_a(early, 1, "bank4")
         stage_c(2, nc.scalar.copy, "bank5")
         stage_c(3, nc.scalar.copy, "bank6")
         scatter_c(2, slice(0, SCALAR_SHARE), scalar_scatter)
-        stage_a(early, 1, "bank4")
         for t in early:
             scatter_a(t, expert_slots(1), scalar_scatter)
-        stage_a([3], 0, "bank4")
         stage_a(late, 1, "bank5")
-        scatter_a(3, slice(0, LAST_CUT), scalar_scatter)
         scatter_a(2, expert_slots(1), scalar_scatter)
         scatter_a(3, slice(LAST_CUT, T), scalar_scatter)
         for t in range(LAST):

@@ -24,13 +24,13 @@ QUADRANTS = 4
 POOL_A, POOL_C = 0, 1
 WINDOW = 704
 LAST_CUT = 128
-SCALAR_SHARE = 160
-PRODUCTS = [slice(256, 384), slice(0, 256), slice(384, 512)]
-SCALAR_COPIES = [slice(256, 384), slice(384, 512)]
-VECTOR_COPIES = [slice(0, 256)]
-PARTS = [slice(256, 384), slice(384, 512), slice(0, 128), slice(128, 256)]
-EMPTIED_BY_VECTOR = [3]
-STORES = {1: slice(256, 512), 3: slice(0, 256)}
+SCALAR_SHARE = 128
+PRODUCTS = [slice(192, 320), slice(0, 192), slice(320, 512)]
+SCALAR_COPIES = [slice(192, 320), slice(320, 448), slice(448, 512)]
+VECTOR_COPIES = [slice(0, 192)]
+PARTS = [slice(192, 320), slice(0, 128), slice(128, 192), slice(320, 448), slice(448, 512)]
+EMPTIED_BY_VECTOR = [3,4]
+STORES = {2: slice(0, 320), 4: slice(320, 512)}
 
 
 def tile_moe_pool_relu_kernel(
@@ -190,10 +190,10 @@ def tile_moe_pool_relu_kernel(
         stage_a([0], 0, "bank0")
         stage_a([1, 2], 0, "bank1")
         stage_a([3], 0, "bank7")
-        scatter_a(2, expert_slots(0), nc.vector.tensor_copy)
+        scatter_a(0, expert_slots(0), nc.vector.tensor_copy)
         for t in early:
             stage_c(t, nc.vector.tensor_copy, f"bank{2 + t}")
-        for t in early:
+        for t in (1, 2):
             scatter_a(t, expert_slots(0), scalar_scatter)
         scatter_a(3, slice(0, LAST_CUT), scalar_scatter)
         stage_a(early, 1, "bank4")

@@ -76,8 +76,8 @@ def tile_moe_pool_relu_kernel(
         token_words = load_words("token_words", x_words[0], nc.scalar, WINDOW)
         codes = {}
         codes[POOL_A, 0] = load_words("wa0_codes", wa_words[0, 0], nc.scalar, H)
-        load_pool_scales(POOL_A, wa_scales, [nc.sync] * QUADRANTS)
-        load_pool_scales(POOL_C, wb_scales, [nc.sync, nc.sync, nc.gpsimd, nc.gpsimd])
+        load_pool_scales(POOL_A, wa_scales, [nc.sync, nc.sync, nc.sync, nc.gpsimd])
+        load_pool_scales(POOL_C, wb_scales, [nc.sync, nc.sync, nc.sync, nc.gpsimd])
         wb_codes = held.tile([P, EXPERTS, H], I32, name="wb_codes", align_bytes=64)
         nc.sync.dma_start(wb_codes[:], wb_words[:, 0].rearrange("e p c d -> p e (c d)").bitcast(I32))
         codes[POOL_A, 1] = load_words("wa1_codes", wa_words[1, 0], nc.sync, H)
@@ -94,7 +94,13 @@ def tile_moe_pool_relu_kernel(
         sorted_words = {(pool, e): {} for pool in (POOL_A, POOL_C) for e in range(EXPERTS)}
         sorted_scales = {POOL_A: {}, POOL_C: {}}
         early, late = [0, 1], [2, 3]
-        sort_columns(nc.scalar.copy, sorted_words[POOL_A, 0], "sorted_wa0", codes[POOL_A, 0][:], U32, early + late)
+        sorted_wa0 = held.tile([P, PACK, P], U32, name="sorted_wa0", align_bytes=64)
+        nc.scalar.copy(
+            sorted_wa0[:].rearrange("k t p -> k p t"),
+            codes[POOL_A, 0][:].bitcast(U32).rearrange("k (p t) -> k p t", t=PACK),
+        )
+        for t in range(PACK):
+            sorted_words[POOL_A, 0][t] = sorted_wa0[:, t, :]
         for planes in ([0], [1, 2], [3]):
             sort_columns(nc.gpsimd.tensor_copy, sorted_scales[POOL_A], "sorted_sa", pool_scales[POOL_A][:], U8, planes)
 

@@ -24,7 +24,7 @@ QUADRANTS = 4
 POOL_A, POOL_C = 0, 1
 WINDOW = 704
 LAST_CUT = 128
-SCALAR_SHARE = 128
+SCALAR_SHARE = 256
 PRODUCTS = [slice(192, 320), slice(0, 192), slice(320, 512)]
 SCALAR_COPIES = [slice(192, 320), slice(320, 448), slice(448, 512)]
 VECTOR_COPIES = [slice(0, 192)]
@@ -101,7 +101,7 @@ def tile_moe_pool_relu_kernel(
         )
         for t in range(PACK):
             sorted_words[POOL_A, 0][t] = sorted_wa0[:, t, :]
-        for planes in ([0], [1, 2], [3]):
+        for planes in ([0], [1], [2], [3]):
             sort_columns(nc.gpsimd.tensor_copy, sorted_scales[POOL_A], "sorted_sa", pool_scales[POOL_A][:], U8, planes)
 
         def sort_wb_words(planes):
@@ -193,15 +193,14 @@ def tile_moe_pool_relu_kernel(
         def product(engine, dst, t, tokens):
             engine.tensor_tensor(dst, by_token[POOL_A, t][:, tokens], by_token[POOL_C, t][:, tokens], MULT)
 
-        stage_a([0], 0, "bank0")
-        stage_a([1, 2], 0, "bank1")
-        stage_a([3], 0, "bank7")
+        for t, tag in enumerate(("bank0", "bank1", "bank7", "bank4")):
+            stage_a([t], 0, tag)
         scatter_a(0, expert_slots(0), nc.vector.tensor_copy)
+        scatter_a(3, slice(0, LAST_CUT), nc.vector.tensor_copy)
         for t in early:
             stage_c(t, nc.vector.tensor_copy, f"bank{2 + t}")
         for t in (1, 2):
             scatter_a(t, expert_slots(0), scalar_scatter)
-        scatter_a(3, slice(0, LAST_CUT), scalar_scatter)
         stage_a(early, 1, "bank4")
         stage_c(2, nc.scalar.copy, "bank5")
         stage_c(3, nc.scalar.copy, "bank6")

@@ -133,14 +133,18 @@ def tile_moe_pool_relu_kernel(
             slot_scales[pool] = held.tile([P, T], U8, name=f"slot_scales{pool}", align_bytes=64)
             slot_words[pool] = held.tile([P, T], U32, name=f"slot_words{pool}", align_bytes=64)
 
-        def gather(pool, slots):
+        def gather_scales(pool, slots):
             nc.vector.tensor_copy(slot_scales[pool][:, slots], token_scales[:].indirect(offsets(pool, slots)))
+
+        def gather_words(pool, slots):
             nc.vector.tensor_copy(slot_words[pool][:, slots], token_words[:].bitcast(U32).indirect(offsets(pool, slots)))
 
         all_slots = slice(0, T)
-        gather(POOL_A, expert_slots(0))
-        gather(POOL_C, all_slots)
-        gather(POOL_A, expert_slots(1))
+        gather_scales(POOL_A, all_slots)
+        gather_words(POOL_A, expert_slots(0))
+        gather_scales(POOL_C, all_slots)
+        gather_words(POOL_C, all_slots)
+        gather_words(POOL_A, expert_slots(1))
 
         by_token = {}
         for t in range(PACK):

@@ -24,7 +24,7 @@ QUADRANTS = 4
 POOL_A, POOL_C = 0, 1
 WINDOW = 704
 LAST_CUT = 128
-SCALAR_SHARE = 256
+SCALAR_SHARE = 160
 PRODUCTS = [slice(192, 320), slice(0, 192), slice(320, 512)]
 SCALAR_COPIES = [slice(192, 320), slice(320, 448), slice(448, 512)]
 VECTOR_COPIES = [slice(0, 192)]
@@ -200,17 +200,17 @@ def tile_moe_pool_relu_kernel(
         for t, tag in enumerate(("bank0", "bank1", "bank7", "bank4")):
             stage_a([t], 0, tag)
         scatter_a(0, expert_slots(0), nc.vector.tensor_copy)
-        scatter_a(3, slice(0, LAST_CUT), nc.vector.tensor_copy)
         for t in early:
             stage_c(t, nc.vector.tensor_copy, f"bank{2 + t}")
         for t in (1, 2):
             scatter_a(t, expert_slots(0), scalar_scatter)
+        scatter_a(3, slice(0, LAST_CUT), scalar_scatter)
         stage_a(early, 1, "bank4")
         stage_c(2, nc.scalar.copy, "bank5")
         stage_c(3, nc.scalar.copy, "bank6")
+        scatter_a(0, expert_slots(1), scalar_scatter)
         scatter_c(2, slice(0, SCALAR_SHARE), scalar_scatter)
-        for t in early:
-            scatter_a(t, expert_slots(1), scalar_scatter)
+        scatter_a(1, expert_slots(1), scalar_scatter)
         stage_a(late, 1, "bank5")
         scatter_a(2, expert_slots(1), scalar_scatter)
         scatter_a(3, slice(LAST_CUT, T), scalar_scatter)

@@ -24,7 +24,7 @@ QUADRANTS = 4
 POOL_A, POOL_C = 0, 1
 WINDOW = 704
 LAST_CUT = 128
-SCALAR_SHARE = 160
+SCALAR_SHARE = 224
 PRODUCTS = [slice(192, 320), slice(0, 192), slice(320, 512)]
 SCALAR_COPIES = [slice(192, 320), slice(320, 448), slice(448, 512)]
 VECTOR_COPIES = [slice(0, 192)]
@@ -173,10 +173,16 @@ def tile_moe_pool_relu_kernel(
         staged_a = held.tile([P, PACK, T], F32, name="staged_a", align_bytes=64)
         staged_c = {}
 
-        def stage_a(planes, e, tag):
+        def scalar_relu(dst, source):
+            nc.scalar.activation(dst, source, RELU)
+
+        def vector_relu(dst, source):
+            nc.vector.tensor_scalar_max(dst, source, 0.0)
+
+        def stage_a(planes, e, tag, relu=scalar_relu):
             acc = sums(POOL_A, [(t, e) for t in planes], tag)
             filled = acc[:, 0 : len(planes) * SLOTS].rearrange("p (t s) -> p t s", s=SLOTS)
-            nc.scalar.activation(staged_a[:, planes[0] : planes[-1] + 1, expert_slots(e)], filled, RELU)
+            relu(staged_a[:, planes[0] : planes[-1] + 1, expert_slots(e)], filled)
 
         def stage_c(t, copy, tag):
             acc = sums(POOL_C, [(t, e) for e in range(EXPERTS)], tag)
@@ -197,8 +203,9 @@ def tile_moe_pool_relu_kernel(
         def product(engine, dst, t, tokens):
             engine.tensor_tensor(dst, by_token[POOL_A, t][:, tokens], by_token[POOL_C, t][:, tokens], MULT)
 
-        for t, tag in enumerate(("bank0", "bank1", "bank7", "bank4")):
+        for t, tag in enumerate(("bank0", "bank1", "bank7")):
             stage_a([t], 0, tag)
+        stage_a([LAST], 0, "bank4", vector_relu)
         scatter_a(0, expert_slots(0), nc.vector.tensor_copy)
         for t in early:
             stage_c(t, nc.vector.tensor_copy, f"bank{2 + t}")

@@ -24,7 +24,8 @@ QUADRANTS = 4
 POOL_A, POOL_C = 0, 1
 WINDOW = 704
 LAST_CUT = 128
-SCALAR_SHARE = 224
+SCALAR_SHARE = 256
+PERIOD = 28
 PRODUCTS = [slice(192, 320), slice(0, 192), slice(320, 512)]
 SCALAR_COPIES = [slice(192, 320), slice(320, 448), slice(448, 512)]
 VECTOR_COPIES = [slice(0, 192)]
@@ -57,30 +58,39 @@ def tile_moe_pool_relu_kernel(
                 queue.dma_start(tile[32 * q : 32 * q + 32, 0:width].bitcast(I32), rows.to_broadcast([8, 4, width // 4]))
             return tile
 
-        pool_scales = []
-        for pool in (POOL_A, POOL_C):
-            tile = held.tile([P, H // 4], I32, name=f"pool_scales{pool}", align_bytes=64)
+        wa_scale_tiles = []
+        for e in range(EXPERTS):
+            tile = held.tile([P, H // 4], I32, name=f"wa_scale_tile{e}", align_bytes=64)
             nc.gpsimd.memset(tile[:], 0)
-            pool_scales.append(tile)
+            wa_scale_tiles.append(tile)
+        wb_scale_tile = held.tile([P, H // 4], I32, name="wb_scale_tile", align_bytes=64)
+        nc.gpsimd.memset(wb_scale_tile[:], 0)
 
-        def load_pool_scales(pool, dram, queues):
+        def load_wa_scales(e):
+            rows = wa_scales[:, 0].rearrange("e b c -> (e b) c")[4 * e : 4 * e + PERIOD, :].bitcast(I32).unsqueeze(0)
+            nc.sync.dma_start(
+                wa_scale_tiles[e][0 : QUADRANTS * PERIOD, :], rows.to_broadcast([QUADRANTS, PERIOD, H // 4])
+            )
+
+        def load_wb_scales(queues):
             for q, queue in enumerate(queues):
                 queue.dma_start(
-                    pool_scales[pool][32 * q : 32 * q + 4 * EXPERTS, :], dram[:, 0, 4 * q : 4 * q + 4, :].bitcast(I32)
+                    wb_scale_tile[32 * q : 32 * q + 4 * EXPERTS, :], wb_scales[:, 0, 4 * q : 4 * q + 4, :].bitcast(I32)
                 )
 
         lists = [held.tile([P, T // 16], U16, name="list_a"), held.tile([P, T // 16], U16, name="list_c")]
         nc.sync.dma_start(lists[POOL_A][:], offs)
         token_scales = load_scales_repeated("token_scales", x_scales[0], [nc.scalar, nc.sync, nc.scalar, nc.sync], WINDOW)
-        nc.sync.dma_start(lists[POOL_C][:], offs2)
+        load_wa_scales(0)
         token_words = load_words("token_words", x_words[0], nc.scalar, WINDOW)
         codes = {}
         codes[POOL_A, 0] = load_words("wa0_codes", wa_words[0, 0], nc.scalar, H)
-        load_pool_scales(POOL_A, wa_scales, [nc.sync, nc.sync, nc.sync, nc.gpsimd])
-        load_pool_scales(POOL_C, wb_scales, [nc.sync, nc.sync, nc.sync, nc.gpsimd])
+        nc.sync.dma_start(lists[POOL_C][:], offs2)
+        load_wb_scales([nc.sync, nc.sync, nc.sync, nc.gpsimd])
         wb_codes = held.tile([P, EXPERTS, H], I32, name="wb_codes", align_bytes=64)
         nc.sync.dma_start(wb_codes[:], wb_words[:, 0].rearrange("e p c d -> p e (c d)").bitcast(I32))
         codes[POOL_A, 1] = load_words("wa1_codes", wa_words[1, 0], nc.sync, H)
+        load_wa_scales(1)
         w2_codes = load_words("w2_codes", w2_words[0], nc.sync, N)
         w2_scale_tile = load_scales_repeated("w2_scale_tile", w2_scales[0], [nc.sync] * QUADRANTS, N)
 
@@ -92,17 +102,18 @@ def tile_moe_pool_relu_kernel(
                 into[t] = tile[:, n, :]
 
         sorted_words = {(pool, e): {} for pool in (POOL_A, POOL_C) for e in range(EXPERTS)}
-        sorted_scales = {POOL_A: {}, POOL_C: {}}
+        sorted_scales = {(POOL_A, 0): {}, (POOL_A, 1): {}, (POOL_C, 0): {}}
+        sorted_scales[POOL_C, 1] = sorted_scales[POOL_C, 0]
+        plane_start = {(POOL_A, 0): 0, (POOL_A, 1): 12, (POOL_C, 0): 0, (POOL_C, 1): 4}
         early, late = [0, 1], [2, 3]
-        sorted_wa0 = held.tile([P, PACK, P], U32, name="sorted_wa0", align_bytes=64)
-        nc.scalar.copy(
-            sorted_wa0[:].rearrange("k t p -> k p t"),
-            codes[POOL_A, 0][:].bitcast(U32).rearrange("k (p t) -> k p t", t=PACK),
-        )
-        for t in range(PACK):
-            sorted_words[POOL_A, 0][t] = sorted_wa0[:, t, :]
-        for planes in ([0], [1], [2], [3]):
-            sort_columns(nc.gpsimd.tensor_copy, sorted_scales[POOL_A], "sorted_sa", pool_scales[POOL_A][:], U8, planes)
+        for planes in (early, late):
+            tile = held.tile([P, len(planes), P], U32, name=f"sorted_wa0_{planes[0]}", align_bytes=64)
+            by_column = codes[POOL_A, 0][:].bitcast(U32).rearrange("k (p t) -> k p t", t=PACK)
+            nc.scalar.copy(tile[:].rearrange("k t p -> k p t"), by_column[:, :, planes[0] : planes[-1] + 1])
+            for n, t in enumerate(planes):
+                sorted_words[POOL_A, 0][t] = tile[:, n, :]
+        for planes in ([0], [1], late):
+            sort_columns(nc.gpsimd.tensor_copy, sorted_scales[POOL_A, 0], "sorted_sa0", wa_scale_tiles[0][:], U8, planes)
 
         def sort_wb_words(planes):
             tile = held.tile([P, EXPERTS, len(planes), P], U32, name=f"sorted_wb_{planes[0]}", align_bytes=64)
@@ -113,14 +124,16 @@ def tile_moe_pool_relu_kernel(
                     sorted_words[POOL_C, e][t] = tile[:, e, n, :]
 
         def sort_wb_scales(planes):
-            sort_columns(nc.gpsimd.tensor_copy, sorted_scales[POOL_C], "sorted_sb", pool_scales[POOL_C][:], U8, planes)
+            sort_columns(nc.gpsimd.tensor_copy, sorted_scales[POOL_C, 0], "sorted_sb", wb_scale_tile[:], U8, planes)
 
         sort_wb_words(early)
         sort_wb_scales(early)
         sort_wb_words(late)
+        sort_columns(nc.gpsimd.tensor_copy, sorted_scales[POOL_A, 1], "sorted_sa1", wa_scale_tiles[1][:], U8, early + late)
         sort_columns(nc.gpsimd.tensor_copy, sorted_words[POOL_A, 1], "sorted_wa1", codes[POOL_A, 1][:], U32, early)
-        sort_wb_scales(late)
+        sort_wb_scales([2])
         sort_columns(nc.gpsimd.tensor_copy, sorted_words[POOL_A, 1], "sorted_wa1", codes[POOL_A, 1][:], U32, late)
+        sort_wb_scales([LAST])
 
         def offsets(pool, slots):
             return lists[pool][:, slots.start // 16 : slots.stop // 16]
@@ -140,11 +153,11 @@ def tile_moe_pool_relu_kernel(
             nc.vector.tensor_copy(slot_words[pool][:, slots], token_words[:].bitcast(U32).indirect(offsets(pool, slots)))
 
         all_slots = slice(0, T)
-        gather_scales(POOL_A, all_slots)
-        gather_words(POOL_A, expert_slots(0))
+        for e in range(EXPERTS):
+            gather_scales(POOL_A, expert_slots(e))
+            gather_words(POOL_A, expert_slots(e))
         gather_scales(POOL_C, all_slots)
         gather_words(POOL_C, all_slots)
-        gather_words(POOL_A, expert_slots(1))
 
         by_token = {}
         for t in range(PACK):
@@ -162,7 +175,7 @@ def tile_moe_pool_relu_kernel(
                 nc.tensor.matmul_mx(
                     out=acc[:, n * SLOTS : (n + 1) * SLOTS],
                     lhsT=sorted_words[pool, e][t].bitcast(FP8X4),
-                    lhsT_scale=sorted_scales[pool][t][4 * e :, :],
+                    lhsT_scale=sorted_scales[pool, e][t][plane_start[pool, e] :, :],
                     rhs=slot_words[pool][:, expert_slots(e)].bitcast(FP8X4),
                     rhs_scale=slot_scales[pool][:, expert_slots(e)],
                     start=True,
@@ -173,16 +186,10 @@ def tile_moe_pool_relu_kernel(
         staged_a = held.tile([P, PACK, T], F32, name="staged_a", align_bytes=64)
         staged_c = {}
 
-        def scalar_relu(dst, source):
-            nc.scalar.activation(dst, source, RELU)
-
-        def vector_relu(dst, source):
-            nc.vector.tensor_scalar_max(dst, source, 0.0)
-
-        def stage_a(planes, e, tag, relu=scalar_relu):
+        def stage_a(planes, e, tag):
             acc = sums(POOL_A, [(t, e) for t in planes], tag)
             filled = acc[:, 0 : len(planes) * SLOTS].rearrange("p (t s) -> p t s", s=SLOTS)
-            relu(staged_a[:, planes[0] : planes[-1] + 1, expert_slots(e)], filled)
+            nc.scalar.activation(staged_a[:, planes[0] : planes[-1] + 1, expert_slots(e)], filled, RELU)
 
         def stage_c(t, copy, tag):
             acc = sums(POOL_C, [(t, e) for e in range(EXPERTS)], tag)
@@ -203,24 +210,25 @@ def tile_moe_pool_relu_kernel(
         def product(engine, dst, t, tokens):
             engine.tensor_tensor(dst, by_token[POOL_A, t][:, tokens], by_token[POOL_C, t][:, tokens], MULT)
 
-        for t, tag in enumerate(("bank0", "bank1", "bank7")):
-            stage_a([t], 0, tag)
-        stage_a([LAST], 0, "bank4", vector_relu)
-        scatter_a(0, expert_slots(0), nc.vector.tensor_copy)
+        stage_a([0], 0, "bank0")
+        stage_a([1], 0, "bank1")
+        scatter_a(0, expert_slots(0), scalar_scatter)
+        stage_a([2], 0, "bank6")
+        stage_a([LAST], 0, "bank7")
+        scatter_a(1, expert_slots(0), nc.vector.tensor_copy)
         for t in early:
             stage_c(t, nc.vector.tensor_copy, f"bank{2 + t}")
-        for t in (1, 2):
-            scatter_a(t, expert_slots(0), scalar_scatter)
-        scatter_a(3, slice(0, LAST_CUT), scalar_scatter)
+        scatter_a(2, expert_slots(0), scalar_scatter)
+        scatter_a(LAST, slice(0, LAST_CUT), scalar_scatter)
         stage_a(early, 1, "bank4")
         stage_c(2, nc.scalar.copy, "bank5")
-        stage_c(3, nc.scalar.copy, "bank6")
         scatter_a(0, expert_slots(1), scalar_scatter)
         scatter_c(2, slice(0, SCALAR_SHARE), scalar_scatter)
+        stage_a(late, 1, "bank4")
         scatter_a(1, expert_slots(1), scalar_scatter)
-        stage_a(late, 1, "bank5")
+        stage_c(LAST, nc.scalar.copy, "bank5")
         scatter_a(2, expert_slots(1), scalar_scatter)
-        scatter_a(3, slice(LAST_CUT, T), scalar_scatter)
+        scatter_a(LAST, slice(LAST_CUT, T), scalar_scatter)
         for t in range(LAST):
             scatter_c(t, slice(SCALAR_SHARE, T) if t == 2 else all_slots, nc.vector.tensor_copy)
             product(nc.gpsimd, side_by_side[:, :, t], t, all_slots)

@@ -24,8 +24,7 @@ QUADRANTS = 4
 POOL_A, POOL_C = 0, 1
 WINDOW = 704
 LAST_CUT = 128
-SCALAR_SHARE = 256
-PERIOD = 28
+SCALAR_SHARE = 224
 PRODUCTS = [slice(192, 320), slice(0, 192), slice(320, 512)]
 SCALAR_COPIES = [slice(192, 320), slice(320, 448), slice(448, 512)]
 VECTOR_COPIES = [slice(0, 192)]
@@ -58,39 +57,30 @@ def tile_moe_pool_relu_kernel(
                 queue.dma_start(tile[32 * q : 32 * q + 32, 0:width].bitcast(I32), rows.to_broadcast([8, 4, width // 4]))
             return tile
 
-        wa_scale_tiles = []
-        for e in range(EXPERTS):
-            tile = held.tile([P, H // 4], I32, name=f"wa_scale_tile{e}", align_bytes=64)
+        pool_scales = []
+        for pool in (POOL_A, POOL_C):
+            tile = held.tile([P, H // 4], I32, name=f"pool_scales{pool}", align_bytes=64)
             nc.gpsimd.memset(tile[:], 0)
-            wa_scale_tiles.append(tile)
-        wb_scale_tile = held.tile([P, H // 4], I32, name="wb_scale_tile", align_bytes=64)
-        nc.gpsimd.memset(wb_scale_tile[:], 0)
+            pool_scales.append(tile)
 
-        def load_wa_scales(e):
-            rows = wa_scales[:, 0].rearrange("e b c -> (e b) c")[4 * e : 4 * e + PERIOD, :].bitcast(I32).unsqueeze(0)
-            nc.sync.dma_start(
-                wa_scale_tiles[e][0 : QUADRANTS * PERIOD, :], rows.to_broadcast([QUADRANTS, PERIOD, H // 4])
-            )
-
-        def load_wb_scales(queues):
+        def load_pool_scales(pool, dram, queues):
             for q, queue in enumerate(queues):
                 queue.dma_start(
-                    wb_scale_tile[32 * q : 32 * q + 4 * EXPERTS, :], wb_scales[:, 0, 4 * q : 4 * q + 4, :].bitcast(I32)
+                    pool_scales[pool][32 * q : 32 * q + 4 * EXPERTS, :], dram[:, 0, 4 * q : 4 * q + 4, :].bitcast(I32)
                 )
 
         lists = [held.tile([P, T // 16], U16, name="list_a"), held.tile([P, T // 16], U16, name="list_c")]
         nc.sync.dma_start(lists[POOL_A][:], offs)
         token_scales = load_scales_repeated("token_scales", x_scales[0], [nc.scalar, nc.sync, nc.scalar, nc.sync], WINDOW)
-        load_wa_scales(0)
+        nc.sync.dma_start(lists[POOL_C][:], offs2)
         token_words = load_words("token_words", x_words[0], nc.scalar, WINDOW)
         codes = {}
         codes[POOL_A, 0] = load_words("wa0_codes", wa_words[0, 0], nc.scalar, H)
-        nc.sync.dma_start(lists[POOL_C][:], offs2)
-        load_wb_scales([nc.sync, nc.sync, nc.sync, nc.gpsimd])
+        load_pool_scales(POOL_A, wa_scales, [nc.sync, nc.sync, nc.sync, nc.gpsimd])
+        load_pool_scales(POOL_C, wb_scales, [nc.sync, nc.sync, nc.sync, nc.gpsimd])
         wb_codes = held.tile([P, EXPERTS, H], I32, name="wb_codes", align_bytes=64)
         nc.sync.dma_start(wb_codes[:], wb_words[:, 0].rearrange("e p c d -> p e (c d)").bitcast(I32))
         codes[POOL_A, 1] = load_words("wa1_codes", wa_words[1, 0], nc.sync, H)
-        load_wa_scales(1)
         w2_codes = load_words("w2_codes", w2_words[0], nc.sync, N)
         w2_scale_tile = load_scales_repeated("w2_scale_tile", w2_scales[0], [nc.sync] * QUADRANTS, N)
 
@@ -102,9 +92,7 @@ def tile_moe_pool_relu_kernel(
                 into[t] = tile[:, n, :]
 
         sorted_words = {(pool, e): {} for pool in (POOL_A, POOL_C) for e in range(EXPERTS)}
-        sorted_scales = {(POOL_A, 0): {}, (POOL_A, 1): {}, (POOL_C, 0): {}}
-        sorted_scales[POOL_C, 1] = sorted_scales[POOL_C, 0]
-        plane_start = {(POOL_A, 0): 0, (POOL_A, 1): 12, (POOL_C, 0): 0, (POOL_C, 1): 4}
+        sorted_scales = {POOL_A: {}, POOL_C: {}}
         early, late = [0, 1], [2, 3]
         for planes in (early, late):
             tile = held.tile([P, len(planes), P], U32, name=f"sorted_wa0_{planes[0]}", align_bytes=64)
@@ -113,7 +101,7 @@ def tile_moe_pool_relu_kernel(
             for n, t in enumerate(planes):
                 sorted_words[POOL_A, 0][t] = tile[:, n, :]
         for planes in ([0], [1], late):
-            sort_columns(nc.gpsimd.tensor_copy, sorted_scales[POOL_A, 0], "sorted_sa0", wa_scale_tiles[0][:], U8, planes)
+            sort_columns(nc.gpsimd.tensor_copy, sorted_scales[POOL_A], "sorted_sa", pool_scales[POOL_A][:], U8, planes)
 
         def sort_wb_words(planes):
             tile = held.tile([P, EXPERTS, len(planes), P], U32, name=f"sorted_wb_{planes[0]}", align_bytes=64)
@@ -124,12 +112,11 @@ def tile_moe_pool_relu_kernel(
                     sorted_words[POOL_C, e][t] = tile[:, e, n, :]
 
         def sort_wb_scales(planes):
-            sort_columns(nc.gpsimd.tensor_copy, sorted_scales[POOL_C, 0], "sorted_sb", wb_scale_tile[:], U8, planes)
+            sort_columns(nc.gpsimd.tensor_copy, sorted_scales[POOL_C], "sorted_sb", pool_scales[POOL_C][:], U8, planes)
 
         sort_wb_words(early)
         sort_wb_scales(early)
         sort_wb_words(late)
-        sort_columns(nc.gpsimd.tensor_copy, sorted_scales[POOL_A, 1], "sorted_sa1", wa_scale_tiles[1][:], U8, early + late)
         sort_columns(nc.gpsimd.tensor_copy, sorted_words[POOL_A, 1], "sorted_wa1", codes[POOL_A, 1][:], U32, early)
         sort_wb_scales([2])
         sort_columns(nc.gpsimd.tensor_copy, sorted_words[POOL_A, 1], "sorted_wa1", codes[POOL_A, 1][:], U32, late)
@@ -153,11 +140,12 @@ def tile_moe_pool_relu_kernel(
             nc.vector.tensor_copy(slot_words[pool][:, slots], token_words[:].bitcast(U32).indirect(offsets(pool, slots)))
 
         all_slots = slice(0, T)
-        for e in range(EXPERTS):
-            gather_scales(POOL_A, expert_slots(e))
-            gather_words(POOL_A, expert_slots(e))
+        gather_scales(POOL_A, expert_slots(0))
+        gather_words(POOL_A, expert_slots(0))
         gather_scales(POOL_C, all_slots)
         gather_words(POOL_C, all_slots)
+        gather_scales(POOL_A, expert_slots(1))
+        gather_words(POOL_A, expert_slots(1))
 
         by_token = {}
         for t in range(PACK):
@@ -175,7 +163,7 @@ def tile_moe_pool_relu_kernel(
                 nc.tensor.matmul_mx(
                     out=acc[:, n * SLOTS : (n + 1) * SLOTS],
                     lhsT=sorted_words[pool, e][t].bitcast(FP8X4),
-                    lhsT_scale=sorted_scales[pool, e][t][plane_start[pool, e] :, :],
+                    lhsT_scale=sorted_scales[pool][t][4 * e :, :],
                     rhs=slot_words[pool][:, expert_slots(e)].bitcast(FP8X4),
                     rhs_scale=slot_scales[pool][:, expert_slots(e)],
                     start=True,

@@ -24,7 +24,7 @@ QUADRANTS = 4
 POOL_A, POOL_C = 0, 1
 WINDOW = 704
 LAST_CUT = 128
-SCALAR_SHARE = 224
+SCALAR_SHARE = 256
 PRODUCTS = [slice(192, 320), slice(0, 192), slice(320, 512)]
 SCALAR_COPIES = [slice(192, 320), slice(320, 448), slice(448, 512)]
 VECTOR_COPIES = [slice(0, 192)]
@@ -140,11 +140,10 @@ def tile_moe_pool_relu_kernel(
             nc.vector.tensor_copy(slot_words[pool][:, slots], token_words[:].bitcast(U32).indirect(offsets(pool, slots)))
 
         all_slots = slice(0, T)
-        gather_scales(POOL_A, expert_slots(0))
+        gather_scales(POOL_A, all_slots)
         gather_words(POOL_A, expert_slots(0))
         gather_scales(POOL_C, all_slots)
         gather_words(POOL_C, all_slots)
-        gather_scales(POOL_A, expert_slots(1))
         gather_words(POOL_A, expert_slots(1))
 
         by_token = {}
@@ -174,10 +173,16 @@ def tile_moe_pool_relu_kernel(
         staged_a = held.tile([P, PACK, T], F32, name="staged_a", align_bytes=64)
         staged_c = {}
 
-        def stage_a(planes, e, tag):
+        def scalar_relu(dst, source):
+            nc.scalar.activation(dst, source, RELU)
+
+        def vector_relu(dst, source):
+            nc.vector.tensor_scalar_max(dst, source, 0.0)
+
+        def stage_a(planes, e, tag, relu=scalar_relu):
             acc = sums(POOL_A, [(t, e) for t in planes], tag)
             filled = acc[:, 0 : len(planes) * SLOTS].rearrange("p (t s) -> p t s", s=SLOTS)
-            nc.scalar.activation(staged_a[:, planes[0] : planes[-1] + 1, expert_slots(e)], filled, RELU)
+            relu(staged_a[:, planes[0] : planes[-1] + 1, expert_slots(e)], filled)
 
         def stage_c(t, copy, tag):
             acc = sums(POOL_C, [(t, e) for e in range(EXPERTS)], tag)
@@ -201,13 +206,13 @@ def tile_moe_pool_relu_kernel(
         stage_a([0], 0, "bank0")
         stage_a([1], 0, "bank1")
         scatter_a(0, expert_slots(0), scalar_scatter)
+        stage_a([LAST], 0, "bank7", vector_relu)
         stage_a([2], 0, "bank6")
-        stage_a([LAST], 0, "bank7")
         scatter_a(1, expert_slots(0), nc.vector.tensor_copy)
         for t in early:
             stage_c(t, nc.vector.tensor_copy, f"bank{2 + t}")
-        scatter_a(2, expert_slots(0), scalar_scatter)
         scatter_a(LAST, slice(0, LAST_CUT), scalar_scatter)
+        scatter_a(2, expert_slots(0), scalar_scatter)
         stage_a(early, 1, "bank4")
         stage_c(2, nc.scalar.copy, "bank5")
         scatter_a(0, expert_slots(1), scalar_scatter)

@@ -114,12 +114,14 @@ def tile_moe_pool_relu_kernel(
         def sort_wb_scales(planes):
             sort_columns(nc.gpsimd.tensor_copy, sorted_scales[POOL_C], "sorted_sb", pool_scales[POOL_C][:], U8, planes)
 
-        sort_wb_words(early)
         sort_wb_scales(early)
-        sort_wb_words(late)
+        sort_wb_words([0])
+        sort_wb_words([1])
+        sort_wb_words([2])
         sort_columns(nc.gpsimd.tensor_copy, sorted_words[POOL_A, 1], "sorted_wa1", codes[POOL_A, 1][:], U32, early)
         sort_wb_scales([2])
         sort_columns(nc.gpsimd.tensor_copy, sorted_words[POOL_A, 1], "sorted_wa1", codes[POOL_A, 1][:], U32, late)
+        sort_wb_words([LAST])
         sort_wb_scales([LAST])
 
         def offsets(pool, slots):

from contextlib import ExitStack

import concourse.mybir as mybir

K, T, H, N = 512, 512, 512, 128
EXPERTS, SLOTS = 2, 256
FLOPS = 2 * (2 * K * H * T) + 2 * H * N * T

F32 = mybir.dt.float32
BF16 = mybir.dt.bfloat16
I32 = mybir.dt.int32
U32 = mybir.dt.uint32
U16 = mybir.dt.uint16
U8 = mybir.dt.uint8
FP8X4 = mybir.dt.float8_e4m3fn_x4
RELU = mybir.ActivationFunctionType.Relu
COPY = mybir.ActivationFunctionType.Copy
MULT = mybir.AluOpType.mult

P = 128
PACK = 4
LAST = PACK - 1
QUADRANTS = 4
POOL_A, POOL_C = 0, 1
WINDOW = 704
LAST_CUT = 128
SCALAR_SHARE = 256
PRODUCTS = [slice(192, 320), slice(0, 192), slice(320, 512)]
SCALAR_COPIES = [slice(192, 320), slice(320, 448), slice(448, 512)]
VECTOR_COPIES = [slice(0, 192)]
PARTS = [slice(192, 320), slice(0, 128), slice(128, 192), slice(320, 448), slice(448, 512)]
EMPTIED_BY_VECTOR = [3,4]
STORES = {2: slice(0, 320), 4: slice(320, 512)}


def tile_moe_pool_relu_kernel(
    tc, x_words, x_scales, wa_words, wa_scales, wb_words, wb_scales, w2_words, w2_scales, offs, offs2, out
):
    nc = tc.nc
    with ExitStack() as ctx:
        held = ctx.enter_context(tc.tile_pool(name="held", bufs=1))
        banks = ctx.enter_context(tc.psum_pool(name="banks", bufs=1))

        def as_words(dram):
            return dram.rearrange("p c d -> p (c d)").bitcast(I32)

        def load_words(name, dram, queue, tile_width):
            tile = held.tile([P, tile_width], I32, name=name, align_bytes=64)
            queue.dma_start(tile[:, 0 : dram.shape[1]], as_words(dram))
            return tile

        def load_scales_repeated(name, dram, queues, tile_width):
            width = dram.shape[1]
            tile = held.tile([P, tile_width], U8, name=name, align_bytes=64)
            for q, queue in enumerate(queues):
                rows = dram[4 * q : 4 * q + 4, :].bitcast(I32).unsqueeze(0)
                queue.dma_start(tile[32 * q : 32 * q + 32, 0:width].bitcast(I32), rows.to_broadcast([8, 4, width // 4]))
            return tile

        pool_scales = []
        for pool in (POOL_A, POOL_C):
            tile = held.tile([P, H // 4], I32, name=f"pool_scales{pool}", align_bytes=64)
            nc.gpsimd.memset(tile[:], 0)
            pool_scales.append(tile)

        def load_pool_scales(pool, dram, queues):
            for q, queue in enumerate(queues):
                queue.dma_start(
                    pool_scales[pool][32 * q : 32 * q + 4 * EXPERTS, :], dram[:, 0, 4 * q : 4 * q + 4, :].bitcast(I32)
                )

        lists = [held.tile([P, T // 16], U16, name="list_a"), held.tile([P, T // 16], U16, name="list_c")]
        nc.sync.dma_start(lists[POOL_A][:], offs)
        token_scales = load_scales_repeated("token_scales", x_scales[0], [nc.scalar, nc.sync, nc.scalar, nc.sync], WINDOW)
        nc.sync.dma_start(lists[POOL_C][:], offs2)
        token_words = load_words("token_words", x_words[0], nc.scalar, WINDOW)
        codes = {}
        codes[POOL_A, 0] = load_words("wa0_codes", wa_words[0, 0], nc.scalar, H)
        load_pool_scales(POOL_A, wa_scales, [nc.sync, nc.sync, nc.sync, nc.gpsimd])
        load_pool_scales(POOL_C, wb_scales, [nc.sync, nc.sync, nc.sync, nc.gpsimd])
        wb_codes = held.tile([P, EXPERTS, H], I32, name="wb_codes", align_bytes=64)
        nc.sync.dma_start(wb_codes[:], wb_words[:, 0].rearrange("e p c d -> p e (c d)").bitcast(I32))
        codes[POOL_A, 1] = load_words("wa1_codes", wa_words[1, 0], nc.sync, H)
        w2_codes = load_words("w2_codes", w2_words[0], nc.sync, N)
        w2_scale_tile = load_scales_repeated("w2_scale_tile", w2_scales[0], [nc.sync] * QUADRANTS, N)

        def sort_columns(copy, into, name, source, dtype, planes):
            tile = held.tile([P, len(planes), P], dtype, name=f"{name}_{planes[0]}", align_bytes=64)
            by_plane = source.bitcast(dtype).rearrange("k (p t) -> k t p", t=PACK)
            copy(tile[:], by_plane[:, planes[0] : planes[-1] + 1, :])
            for n, t in enumerate(planes):
                into[t] = tile[:, n, :]

        sorted_words = {(pool, e): {} for pool in (POOL_A, POOL_C) for e in range(EXPERTS)}
        sorted_scales = {POOL_A: {}, POOL_C: {}}
        early, late = [0, 1], [2, 3]
        for planes in (early, late):
            tile = held.tile([P, len(planes), P], U32, name=f"sorted_wa0_{planes[0]}", align_bytes=64)
            by_column = codes[POOL_A, 0][:].bitcast(U32).rearrange("k (p t) -> k p t", t=PACK)
            nc.scalar.copy(tile[:].rearrange("k t p -> k p t"), by_column[:, :, planes[0] : planes[-1] + 1])
            for n, t in enumerate(planes):
                sorted_words[POOL_A, 0][t] = tile[:, n, :]
        for planes in ([0], [1], late):
            sort_columns(nc.gpsimd.tensor_copy, sorted_scales[POOL_A], "sorted_sa", pool_scales[POOL_A][:], U8, planes)

        def sort_wb_words(planes):
            tile = held.tile([P, EXPERTS, len(planes), P], U32, name=f"sorted_wb_{planes[0]}", align_bytes=64)
            by_plane = wb_codes[:].bitcast(U32).rearrange("k e (p t) -> k e t p", t=PACK)
            nc.gpsimd.tensor_copy(tile[:], by_plane[:, :, planes[0] : planes[-1] + 1, :])
            for e in range(EXPERTS):
                for n, t in enumerate(planes):
                    sorted_words[POOL_C, e][t] = tile[:, e, n, :]

        def sort_wb_scales(planes):
            sort_columns(nc.gpsimd.tensor_copy, sorted_scales[POOL_C], "sorted_sb", pool_scales[POOL_C][:], U8, planes)

        sort_wb_scales(early)
        sort_wb_words([0])
        sort_wb_words([1])
        sort_wb_words([2])
        sort_columns(nc.gpsimd.tensor_copy, sorted_words[POOL_A, 1], "sorted_wa1", codes[POOL_A, 1][:], U32, early)
        sort_wb_scales([2])
        sort_columns(nc.gpsimd.tensor_copy, sorted_words[POOL_A, 1], "sorted_wa1", codes[POOL_A, 1][:], U32, late)
        sort_wb_words([LAST])
        sort_wb_scales([LAST])

        def offsets(pool, slots):
            return lists[pool][:, slots.start // 16 : slots.stop // 16]

        def expert_slots(e):
            return slice(e * SLOTS, (e + 1) * SLOTS)

        slot_words, slot_scales = {}, {}
        for pool in (POOL_A, POOL_C):
            slot_scales[pool] = held.tile([P, T], U8, name=f"slot_scales{pool}", align_bytes=64)
            slot_words[pool] = held.tile([P, T], U32, name=f"slot_words{pool}", align_bytes=64)

        def gather_scales(pool, slots):
            nc.vector.tensor_copy(slot_scales[pool][:, slots], token_scales[:].indirect(offsets(pool, slots)))

        def gather_words(pool, slots):
            nc.vector.tensor_copy(slot_words[pool][:, slots], token_words[:].bitcast(U32).indirect(offsets(pool, slots)))

        all_slots = slice(0, T)
        gather_scales(POOL_A, all_slots)
        gather_words(POOL_A, expert_slots(0))
        gather_scales(POOL_C, all_slots)
        gather_words(POOL_C, all_slots)
        gather_words(POOL_A, expert_slots(1))

        by_token = {}
        for t in range(PACK):
            by_token[POOL_A, t] = held.tile([P, T], F32, name=f"a_by_token{t}", align_bytes=64)

        def open_window(t, tag):
            by_token[POOL_C, t] = held.tile([P, WINDOW], F32, name=f"c_by_token{t}", tag=tag, align_bytes=64)

        for t in range(LAST):
            open_window(t, f"window_c{t}")

        def sums(pool, pieces, tag):
            acc = banks.tile([P, T], F32, name="acc", tag=tag)
            for n, (t, e) in enumerate(pieces):
                nc.tensor.matmul_mx(
                    out=acc[:, n * SLOTS : (n + 1) * SLOTS],
                    lhsT=sorted_words[pool, e][t].bitcast(FP8X4),
                    lhsT_scale=sorted_scales[pool][t][4 * e :, :],
                    rhs=slot_words[pool][:, expert_slots(e)].bitcast(FP8X4),
                    rhs_scale=slot_scales[pool][:, expert_slots(e)],
                    start=True,
                    stop=True,
                )
            return acc

        staged_a = held.tile([P, PACK, T], F32, name="staged_a", align_bytes=64)
        staged_c = {}

        def scalar_relu(dst, source):
            nc.scalar.activation(dst, source, RELU)

        def vector_relu(dst, source):
            nc.vector.tensor_scalar_max(dst, source, 0.0)

        def stage_a(planes, e, tag, relu=scalar_relu):
            acc = sums(POOL_A, [(t, e) for t in planes], tag)
            filled = acc[:, 0 : len(planes) * SLOTS].rearrange("p (t s) -> p t s", s=SLOTS)
            relu(staged_a[:, planes[0] : planes[-1] + 1, expert_slots(e)], filled)

        def stage_c(t, copy, tag):
            acc = sums(POOL_C, [(t, e) for e in range(EXPERTS)], tag)
            staged_c[t] = held.tile([P, T], F32, name=f"staged_c{t}", align_bytes=64)
            copy(staged_c[t][:], acc[:])

        def scalar_scatter(window, source):
            nc.scalar.activation(window, source, COPY)

        def scatter_a(t, slots, copy):
            copy(by_token[POOL_A, t][:].indirect(offsets(POOL_A, slots)), staged_a[:, t, slots])

        def scatter_c(t, slots, copy):
            copy(by_token[POOL_C, t][:].indirect(offsets(POOL_C, slots)), staged_c[t][:, slots])

        side_by_side = held.tile([P, T, PACK], BF16, name="side_by_side", align_bytes=64)

        def product(engine, dst, t, tokens):
            engine.tensor_tensor(dst, by_token[POOL_A, t][:, tokens], by_token[POOL_C, t][:, tokens], MULT)

        stage_a([0], 0, "bank0")
        stage_a([1], 0, "bank1")
        scatter_a(0, expert_slots(0), scalar_scatter)
        stage_a([LAST], 0, "bank7", vector_relu)
        stage_a([2], 0, "bank6")
        scatter_a(1, expert_slots(0), nc.vector.tensor_copy)
        for t in early:
            stage_c(t, nc.vector.tensor_copy, f"bank{2 + t}")
        scatter_a(LAST, slice(0, LAST_CUT), scalar_scatter)
        scatter_a(2, expert_slots(0), scalar_scatter)
        stage_a(early, 1, "bank4")
        stage_c(2, nc.scalar.copy, "bank5")
        scatter_a(0, expert_slots(1), scalar_scatter)
        scatter_c(2, slice(0, SCALAR_SHARE), scalar_scatter)
        stage_a(late, 1, "bank4")
        scatter_a(1, expert_slots(1), scalar_scatter)
        stage_c(LAST, nc.scalar.copy, "bank5")
        scatter_a(2, expert_slots(1), scalar_scatter)
        scatter_a(LAST, slice(LAST_CUT, T), scalar_scatter)
        for t in range(LAST):
            scatter_c(t, slice(SCALAR_SHARE, T) if t == 2 else all_slots, nc.vector.tensor_copy)
            product(nc.gpsimd, side_by_side[:, :, t], t, all_slots)
        open_window(LAST, "window_c0")
        scatter_c(LAST, all_slots, nc.vector.tensor_copy)

        last_plane = held.tile([P, T], BF16, name="last_plane", tag=f"window_c{LAST - 1}", align_bytes=64)
        for tokens in PRODUCTS:
            product(nc.vector, last_plane[:, tokens], LAST, tokens)
        for tokens in SCALAR_COPIES:
            nc.scalar.copy(side_by_side[:, tokens, LAST], last_plane[:, tokens])
        for tokens in VECTOR_COPIES:
            nc.vector.tensor_copy(side_by_side[:, tokens, LAST], last_plane[:, tokens])

        h_words = held.tile([P, T], U32, name="h_words", align_bytes=64)
        h_scales = held.tile([P, T], U8, name="h_scales", align_bytes=64)
        result = held.tile([N, T], F32, name="result")
        for u, tokens in enumerate(PARTS):
            nc.vector.quantize_mx(
                out=h_words[:, tokens].bitcast(FP8X4),
                scales=h_scales[:, tokens],
                in_=side_by_side[:, tokens, :].rearrange("p c t -> p (c t)"),
            )
            total = banks.tile([N, tokens.stop - tokens.start], F32, name="total", tag=f"bank{u}")
            nc.tensor.matmul_mx(
                out=total[:],
                lhsT=w2_codes[:].bitcast(FP8X4),
                lhsT_scale=w2_scale_tile[:],
                rhs=h_words[:, tokens].bitcast(FP8X4),
                rhs_scale=h_scales[:, tokens],
                start=True,
                stop=True,
            )
            if u in EMPTIED_BY_VECTOR:
                nc.vector.tensor_copy(result[:, tokens], total[:])
            else:
                nc.scalar.copy(result[:, tokens], total[:])
            if u in STORES:
                nc.sync.dma_start(out[:, STORES[u]], result[:, STORES[u]])
